import numpy as np, ml_dtypes
CORES = [1,5,17,21,33,37,49,53]
N = 8
import mx_ref
BF = ml_dtypes.bfloat16
def pick(q, e):
    c = np.concatenate([q[0].reshape(128, -1, 4), np.zeros((128, 1, 4), np.uint8)], axis=1); s = np.concatenate([q[1], np.ones((16, 1), np.uint8)], axis=1)
    return (np.ascontiguousarray(c[:, e].reshape(128, -1)), np.ascontiguousarray(s[:, e]))
def join(*qs):
    return (np.concatenate([q[0] for q in qs], axis=1), np.concatenate([q[1] for q in qs], axis=1))
def put(q, e, v):
    c, s = q[0].reshape(128, -1, 4).copy(), q[1].copy(); c[:, e] = v[0].reshape(128, -1, 4); s[:, e] = v[1]
    return (c.reshape(128, -1), s)
def pk(c, s):
    return (np.ascontiguousarray(c), mx_ref.live(s))
def emit(q):
    return q[0], q[1]
def cols(t, e):
    v = np.concatenate([t.reshape(128, -1, 4), np.zeros((128, 1, 4), BF)], axis=1)
    return np.ascontiguousarray(v[:, e]).reshape(128, -1)
def cut(t, i, w=512):
    return t[:, w * i:w * i + w]
def decode(q):
    o = []
    for b in range(4):
        e = np.zeros((128, 128, 4), np.float32); e[np.arange(128), np.arange(128), b] = 1
        o.append(mx_ref.matmul(mx_ref.quantize(e.reshape(128, 512).astype(BF)), q))
    return np.stack(o, axis=2).reshape(128, -1)
def f(rng, *shape):
    return mx_ref.flush((rng.standard_normal(shape, dtype=np.float32) * np.exp2(rng.integers(-2, 3, shape[:-1] + (1,)))).astype(BF))
def wide(rng, *shape, cols=0):
    v = rng.standard_normal(shape, dtype=np.float32) * np.exp2(rng.integers(-12, 13, shape)).astype(np.float32)
    if cols: v *= np.repeat(np.exp2(rng.integers(-cols, cols + 1, shape[:-2] + (1, shape[-1] // 4))) * (rng.random(shape[:-2] + (1, shape[-1] // 4)) > 0.0625), 4, axis=-1).astype(np.float32)
    return mx_ref.flush(v.astype(BF))
G, T, CAPP, R = 16, 96, 48, 3
def fit(v):
    v = np.array(v, np.float32)
    v[np.abs(v) < np.float32(2.0 ** -10)] = 0
    return v.astype(BF)
def plain(rng):
    return {"cb": fit(f(rng, N, 128, 4 * G)), "x": fit(f(rng, N, 128, 4 * R * T)), "w": f(rng, N, 128, 512)}
def part(rng, lab, k):
    s = (128, len(k), 4)
    v = np.where(k[None, :, None] == 2, rng.standard_normal(s), 1 + rng.random(s))
    return (v * (lab[:, None] == k[None, :])[:, :, None]).reshape(128, -1)
def setup_inputs(rng):
    return plain(rng)
def setup_inputs_crowd(rng):
    d = plain(rng)
    lab = rng.permutation(np.repeat([0, 1, 2], [40, 40, 48]))
    q, g = int(rng.integers(0, N - 2)), rng.permutation(G)[:2]
    home = int(rng.integers(0, R))
    rush = (home + 1 + int(rng.integers(0, R - 1))) % R
    cb = np.stack([part(rng, lab, np.full(G, 2)) for r in range(N)])
    k, size = np.zeros(G, int), np.full(G, 2.0 ** -6)
    k[g[1]] = 1
    size[g] = 1
    cb[q] = part(rng, lab, k) * np.repeat(size, 4)
    kinds = np.full((N, R, T), 2)
    for t in range(R):
        three, whole = np.sort(rng.permutation(N)[:3]), -1
        if t == home: three = np.concatenate([[q], np.sort(q + 1 + rng.permutation(N - 1 - q)[:2])])
        if t == rush:
            four, j = np.sort(rng.permutation(N)[:4]), int(rng.integers(0, 3))
            three, whole = np.delete(four, j), int(four[j])
        for s in range(N):
            more = int(rng.integers(1, T // 8 + 1))
            if s == three[0]: e = np.concatenate([np.zeros(CAPP, int), np.ones(more, int)])
            elif s == three[1]: e = np.concatenate([np.zeros(CAPP - 1, int), np.ones(1, int)])
            elif s == three[2]: e = np.concatenate([np.zeros(CAPP - 1, int), np.ones(1, int), rng.integers(0, 2, more)])
            elif s == whole: e = np.concatenate([np.zeros(CAPP, int), np.ones(T - CAPP, int)])
            else: e = np.zeros(int(rng.integers(CAPP // 2, CAPP + T // 8 + 1)), int)
            kinds[s, t, np.sort(rng.permutation(T)[:len(e)])] = e
    d["cb"], d["x"] = fit(cb), fit(np.stack([part(rng, lab, kinds[s].reshape(-1)) for s in range(N)]))
    return d
def setup_inputs_ties(rng):
    d = plain(rng)
    H = G // 2
    shared = fit(rng.standard_normal((128, 4 * H)))
    for r in range(N):
        both = np.concatenate([shared, fit(rng.standard_normal((128, 4 * H)))], axis=1)
        d["cb"][r] = cols(both, rng.permutation(np.concatenate([rng.integers(0, H, G - H), H + np.arange(H)])))
        v = cut(d["x"][r], 0, 4 * T).copy().reshape(128, T, 4)
        at = rng.permutation(T)
        v[:, at[:H]] = shared.reshape(128, H, 4)
        v[:, at[H:H + T // 16]] = 0
        d["x"][r] = np.concatenate([cols(v.reshape(128, -1), rng.permutation(T)) for t in range(R)], axis=1)
    return d
def setup_inputs_full(rng):
    d = plain(rng)
    at = rng.permutation(128)
    own = at[None, :] == np.arange(128)[:, None]
    cb = (1 + rng.random((128, 128, 4))) * np.where(own, 1.0, 2.0 ** -8)[:, :, None]
    kinds, who = np.zeros((N, R, T), int), np.arange(128) // G
    least, below = [], []
    for t in range(R):
        s, q = [int(v) for v in rng.permutation(N)[:2]]
        mine, free = np.flatnonzero(who == q), np.flatnonzero(who != q)
        if t == 0 or t == R - 1:
            least.append(int(rng.choice([v for v in free if G <= v < 128 - G and v not in least])))
            free = free[free != least[-1]]
            below.append((s + 1 + int(rng.integers(0, N - 1))) % N)
        for r in range(N):
            if r == s: kinds[r, t] = rng.permutation(np.concatenate([mine, mine, rng.choice(free, T - 2 * G)]))
            elif r < s: kinds[r, t] = rng.choice(free, T)
            else: kinds[r, t] = rng.choice(np.concatenate([free, mine]), T)
    x = np.zeros((N, 128, R * T, 4))
    for r in range(N):
        k = kinds[r].reshape(-1)
        x[r] = np.where(own[:, k][:, :, None], 1 + rng.random((128, R * T, 4)), (2 * rng.random((128, R * T, 4)) - 1) * 2.0 ** -7)
    x[below[0]][:, :2] = -(1 + rng.random((128, 2, 4))) * np.where(own[:, least[0]], 2.0 ** -9, 2.0 ** -6)[:, None, None]
    size = np.where(own[:, least[1]], 2.0 ** 15, np.where(own[:, least[0]], 2.0 ** 24, 2.0 ** 21))
    i = (R - 1) * T
    x[below[1]][:, i:i + 2] = -(3 + rng.random((128, 2, 4))) * size[:, None, None]
    d["cb"] = fit(np.stack([cb[:, G * r:G * r + G].reshape(128, -1) for r in range(N)]))
    d["x"] = fit(x.reshape(N, 128, -1))
    return d
def setup_inputs_idle(rng):
    d = plain(rng)
    q, own = int(rng.integers(0, N)), rng.permutation(128) < 64
    cb = rng.standard_normal((N, 128, 4 * G))
    for r in range(N): cb[r] *= (own if r == q else ~own)[:, None]
    early = np.arange(4 * R * T) < 4 * (R - 1) * T
    d["cb"], d["x"] = fit(cb), fit(d["x"].astype(np.float32) * ~(own[:, None] & early[None, :]))
    return d
def setup_inputs_spread(rng):
    d = plain(rng)
    d["cb"] = fit(wide(rng, N, 128, 4 * G).astype(np.float32) * 64)
    d["x"] = fit(wide(rng, N, 128, 4 * R * T, cols=4).astype(np.float32) * 64)
    return d
def check_inputs(d):
    b = []
    for k, lo, hi in (("cb", -10, 28), ("x", -10, 28), ("w", -30, 30)):
        v = np.abs(d[k].astype(np.float32))
        if not (np.isfinite(v).all() and ((v == 0) | (v >= 2.0 ** lo) & (v <= 2.0 ** hi)).all()): b.append("a value of " + k)
    return b
def admitted(win):
    a = np.full((2, 128), -1)
    for s in range(N):
        n = np.zeros(N, int)
        for i in range(T):
            k = win[T * s + i]
            n[k // G] += 1
            if n[k // G] > CAPP: continue
            if a[0, k] < 0: a[0, k] = T * s + i
            elif a[1, k] < 0: a[1, k] = T * s + i
    return a
def reference(cb, x, w):
    y, ids = np.zeros((N, 128, R * 2 * G), np.float32), np.zeros((N, 1, R * 2 * G), np.float32)
    oc, osc = np.zeros((N, 128, 4 * G), np.uint8), np.zeros((N, 16, G), np.uint8)
    half, quarter = np.float32(0.5), np.float32(0.25)
    qw = [mx_ref.quantize(np.ascontiguousarray(w[r])) for r in range(N)]
    c = join(*[mx_ref.quantize(np.ascontiguousarray(cb[r])) for r in range(N)])
    for t in range(R):
        tok = join(*[mx_ref.quantize(np.ascontiguousarray(cut(x[s], t, 4 * T))) for s in range(N)])
        a = admitted(np.argmax(mx_ref.matmul(c, tok) + np.float32(0), axis=0))
        for r in range(N):
            e = a[:, G * r:G * r + G].T.reshape(-1)
            i = t * 2 * G
            y[r, :, i:i + 2 * G] = mx_ref.matmul(qw[r], pick(tok, e))
            ids[r, 0, i:i + 2 * G] = e
        v = decode(join(c, pick(tok, a[0]), pick(tok, a[1]))).reshape(128, 3, 128, 4)
        one = half * v[:, 0] + half * v[:, 1]
        two = half * v[:, 0] + (quarter * v[:, 1] + quarter * v[:, 2])
        new = np.where((a[1] >= 0)[None, :, None], two, one).reshape(128, 512).astype(BF)
        moved = np.flatnonzero(a[0] >= 0)
        c = put(c, moved, pick(mx_ref.quantize(np.ascontiguousarray(new)), moved))
    for r in range(N):
        oc[r], osc[r] = emit(pick(c, np.arange(G * r, G * r + G)))
    return {"y": y, "ids": ids, "oc": oc, "osc": osc}

@@ -1,0 +1,469 @@
+from concourse.bass import DstId, RemoteDMATransfer
+from concourse.mybir import dt, AluOpType, AxisListType, ActivationFunctionType
+
+G, TOK, CAPP, R, H = 16, 96, 48, 3, 4
+TW = 544
+BIGW = 16384
+CO = 48
+
+F32, BF, I32, U16, COD, PLN = "float32", "bfloat16", "int32", "uint16", "float8_e4m3fn_x4", "uint8"
+SCRATCH = {"PS": ("psum", [128, 4096], F32)}
+SEMAPHORES = ["vd", "sd", "pd", "gd", "sent"]
+
+
+def _buf(name, n, dtype):
+    SCRATCH[name] = ("sbuf", [128, n], dtype)
+
+
+def _mx(name, n):
+    _buf(name + "c", n, COD)
+    _buf(name + "s", n, PLN)
+
+
+for _n, _w in (("CBT", 512), ("X0", 512), ("X12", 768), ("WT", 512), ("ZT", 704), ("TRT", 512), ("E25", 2048), ("E50", 2048), ("THR", 128), ("KP", 128),
+               ("KO", 128), ("HI", 32), ("LO", 32), ("OT", 512), ("NT", 512), ("NO", 512), ("YF", 32), ("Y", 544), ("NEW", 512), ("J", 512), ("JA", 256)):
+    _buf(_n, _w, BF)
+for _n, _w in (("RM", 128), ("NEG", 128), ("DV", 128), ("TA", 256), ("QC", 1), ("KC", 2), ("RB", 512), ("WV", 4), ("SC", 128), ("CC", 8), ("XA", 16),
+               ("XB", 16), ("MM", 4), ("TT", 4), ("SS", 64), ("HB", 64), ("HC", 64), ("YO", 96), ("SN", 2), ("IB", 2)):
+    _buf(_n, _w, F32)
+for _n, _w in (("QI", 1), ("QJ", 1), ("NV", 96), ("RI", 128)):
+    _buf(_n, _w, I32)
+for _n, _w in (("XQ0", 128), ("XQ12", 192), ("WQ", 128), ("TRQ", 128), ("E25Q", 512), ("E50Q", 512), ("OC", 128), ("NQ", 128), ("NOQ", 128), ("YQ", 136),
+               ("HX0", 96), ("HX12", 192)):
+    _mx(_n, _w)
+for _t in range(R):
+    _mx("TK%d" % _t, TW)
+    _mx("CA%d" % _t, 128)
+    _mx("PP%d" % _t, 32)
+    _mx("PK%d" % _t, 128)
+    _buf("NP%d" % _t, 2, F32)
+    _buf("LN%d" % _t, 2, F32)
+    _buf("KB%d" % _t, 12, F32)
+    _buf("KN%d" % _t, 12, F32)
+    _buf("ID%d" % _t, 2, F32)
+    _buf("OP%d" % _t, 2, U16)
+    _buf("OF%d" % _t, 4, U16)
+    _buf("OS%d" % _t, 2, U16)
+    SEMAPHORES += ["aC%d" % _t, "aT%d" % _t, "aL%d" % _t, "aK%d" % _t, "hc%d" % _t, "hs%d" % _t]
+for _t in range(R + 1):
+    _mx("HW%d" % _t, 192)
+SEMAPHORES += ["d%d" % _i for _i in range(30)]
+
+
+def _bits(es):
+    return sum(1 << e for e in es)
+
+
+def _helper_of(core, T, topo):
+    return [c for c in topo.cores_of(core) if T.rank_of(c) is None and topo.die(c) == topo.die(core)][0]
+
+
+def _half(r):
+    return list(range(H * (r // H), H * (r // H) + H))
+
+
+def _base(r):
+    return 0 if r < H else 32
+
+
+def _land(r):
+    return 4 * TOK + 32 if r < H else 0
+
+
+def _dst(c, topo):
+    a = topo.addr(c)
+    return DstId(rid=a[0], pnc=a[1])
+
+
+def _relay(t):
+    return ("HX0", 0) if t == 0 else ("HX12", TOK * (t - 1))
+
+
+def _near_engines(a, b, far, topo):
+    return [e for e in topo.engines(a, b) if e not in topo.engines(a, far)]
+
+
+def _helper(g, core, rank, T, topo):
+    me = T.cores[rank]
+    far = [r for r in _half(rank) if topo.chip(T.cores[r]) != topo.chip(me)]
+    es = topo.engines(core, T.cores[far[0]])
+    came = len(_near_engines(me, core, T.cores[far[0]], topo)) // 2
+    n = 0
+    for t in range(R):
+        for k in "cs":
+            g.wait_ge(T.sem["h%s%d" % (k, t)], came)
+            dsts = []
+            for r in far:
+                o = _base(r) + TOK * (rank % H)
+                v = T["TK%d%s" % (t, k)][:, o:o + TOK]
+                dsts.append(v.bitcast(dt.uint8) if k == "c" else v)
+            nm, a = _relay(t)
+            v = T[nm + k][:, a:a + TOK]
+            src = v.bitcast(dt.uint8) if k == "c" else v
+            g.remote_dma_fused([RemoteDMATransfer(dst_ids=[_dst(T.cores[r], topo) for r in far], dma_engine_mask=_bits(es),
+                                                  remote_sem=T.sem["aT%d" % t], srcs=[src], dsts=dsts)], local_sem=T.sem.sent)
+            n += len(es)
+    g.wait_ge(T.sem.sent, n)
+
+
+def rank_program(g, core, T, topo):
+    rank = T.rank_of(core)
+    if rank is None:
+        for r in range(len(T.cores)):
+            if _helper_of(T.cores[r], T, topo) == core:
+                _helper(g, core, r, T, topo)
+        return
+    AL, AF, AX = AluOpType, ActivationFunctionType, AxisListType.X
+    half, sl = rank // H, rank % H
+    part = (rank + H) % (2 * H)
+    own = (rank, part)
+    tb, lb = _base(rank), _land(rank)
+    zo = tb + 4 * TOK + (64 if half == 0 else 0)
+    up = 64 if half == 0 else 0
+    eng = {"v": g.vector, "s": g.scalar, "p": g.tensor, "g": g, "y": g.sync}
+    done = {"v": "vd", "s": "sd", "p": "pd", "g": "gd"}
+    cnt, seen, log, nd = {}, {}, {}, [0]
+
+    def cols(x):
+        nm, a, b = x[0], x[1], x[2]
+        st = x[3] if len(x) > 3 else 1
+        if nm == "PS":
+            return nm, frozenset(range(a // 512, (b - 1) // 512 + 1))
+        return nm, frozenset(range(a, b, st))
+
+    def view(x):
+        st = x[3] if len(x) > 3 else 1
+        return T[x[0]][:, x[1]:x[2]] if st == 1 else T[x[0]][:, x[1]:x[2]:st]
+
+    def wait(q, tok):
+        if seen.get((q, tok[0]), 0) < tok[1]:
+            eng[q].wait_ge(T.sem[tok[0]], tok[1])
+            seen[(q, tok[0])] = tok[1]
+
+    def before(q, rd, wr):
+        best = {}
+        for kind, xs in (("r", rd), ("w", wr)):
+            for x in xs:
+                nm, cs = cols(x)
+                for k, c2, tok, q2 in log.get(nm, []):
+                    if (kind == "w" or k == "w") and cs & c2 and not (q == "p" and q2 == "p"):
+                        best[tok[0]] = max(best.get(tok[0], 0), tok[1])
+        for s in sorted(best):
+            wait(q, (s, best[s]))
+
+    def after(q, tok, rd, wr):
+        for x in wr:
+            nm, cs = cols(x)
+            log[nm] = [e for e in log.get(nm, []) if not e[1] <= cs] + [("w", cs, tok, q)]
+        for x in rd:
+            nm, cs = cols(x)
+            log.setdefault(nm, []).append(("r", cs, tok, q))
+
+    def op(q, f, rd, wr):
+        before(q, rd, wr)
+        cnt[q] = cnt.get(q, 0) + 1
+        tok = (done[q], cnt[q])
+        f(eng[q]).then_inc(T.sem[tok[0]], 1)
+        after(q, tok, rd, wr)
+        return tok
+
+    def isap(x):
+        return isinstance(x, tuple)
+
+    def ts(out, in0, s1, op0, s2=None, op1=None):
+        sc = [view(s) if isap(s) else s for s in (s1, s2)]
+        rd = [in0] + [s for s in (s1, s2) if isap(s)]
+        if op1 is None:
+            return op("v", lambda v: v.tensor_scalar(view(out), view(in0), sc[0], None, op0), rd, [out])
+        return op("v", lambda v: v.tensor_scalar(view(out), view(in0), sc[0], sc[1], op0, op1), rd, [out])
+
+    def tt(out, a, b, o):
+        return op("v", lambda v: v.tensor_tensor(view(out), view(a), view(b), o), [a, b], [out])
+
+    def cp(out, a):
+        return op("v", lambda v: v.tensor_copy(view(out), view(a)), [a], [out])
+
+    def act(out, a, f, bias=0.0, scale=1.0, acc=None):
+        rd = [a] + ([bias] if isap(bias) else [])
+        b = view(bias) if isap(bias) else bias
+        if acc is not None:
+            return op("s", lambda s: s.activation(view(out), view(a), f, bias=b, scale=scale, accum_out=view(acc)), rd, [out, acc])
+        if f == AF.Copy:
+            return op("s", lambda s: s.activation(view(out), view(a), f, scale=scale), rd, [out])
+        return op("s", lambda s: s.activation(view(out), view(a), f, bias=b, scale=scale), rd, [out])
+
+    def red(out, a, o):
+        return op("v", lambda v: v.tensor_reduce(view(out), view(a), AX, o), [a], [out])
+
+    def fill(x, c):
+        return op("v", lambda v: v.memset(view(x), c), [], [x])
+
+    def scan(out, d0, d1, ini, o0, o1):
+        return op("v", lambda v: v.tensor_tensor_scan(view(out), view(d0), view(d1), ini, o0, o1), [d0, d1], [out])
+
+    def qz(nm, a, n, tile, ta=0):
+        oc, os, i = (nm + "c", a, a + n), (nm + "s", a, a + n), (tile, ta, ta + 4 * n)
+        return op("v", lambda v: v.quantize_mx(view(oc), view(os), view(i)), [i], [oc, os])
+
+    def mm(bank, st, sa, mv, ma, start=True, stop=True):
+        o = ("PS", 512 * bank, 512 * bank + 128)
+        a, b = (st + "c", sa, sa + 128), (st + "s", sa, sa + 128)
+        c, d = (mv + "c", ma, ma + 128), (mv + "s", ma, ma + 128)
+        return op("p", lambda p: p.matmul_mx(view(o), view(a), view(b), view(c), view(d), start, stop), [a, b, c, d], [o])
+
+    def pick(dst, da, src, wa, wb, of, oa, ob):
+        n = 16 * (ob - oa)
+        o, w, f = (of, oa, ob), (src + "c", wa, wb), (dst + "c", da, da + n)
+        op("v", lambda v: v.tensor_copy(view(f).bitcast(dt.uint32), view(w).bitcast(dt.uint32).indirect(view(o))), [w, o], [f])
+        w2, f2 = (src + "s", wa, wb), (dst + "s", da, da + n)
+        op("s", lambda s: s.activation(view(f2), view(w2).indirect(view(o)), AF.Copy), [w2, o], [f2])
+
+    def dma(q, out, in_, rd, wr):
+        before(q, rd, wr)
+        tok = ("d%d" % nd[0], 16)
+        nd[0] += 1
+        eng[q].dma_start(out, in_).then_inc(T.sem[tok[0]], 16)
+        after(q, tok, rd, wr)
+
+    def lcopy(q, dst, da, src, sa, n):
+        for k in "cs":
+            i, o = (src + k, sa, sa + n), (dst + k, da, da + n)
+            vi, vo = view(i), view(o)
+            if k == "c":
+                vi, vo = vi.bitcast(dt.uint8), vo.bitcast(dt.uint8)
+            dma(q, vo, vi, [i], [o])
+
+    def ext(sem, val, xs):
+        for x in xs:
+            nm, cs = cols(x)
+            log.setdefault(nm, []).append(("w", cs, (sem, val), "x"))
+
+    peers = [r for r in range(len(T.cores)) if r != rank]
+    near = [r for r in peers if topo.chip(T.cores[r]) == topo.chip(core)]
+    far = [r for r in peers if r not in near]
+    efar = topo.engines(core, T.cores[far[0]])
+    enear = _near_engines(core, T.cores[near[0]], T.cores[far[0]], topo)
+    hn2 = len(enear) // 2
+    sent = [0]
+
+    def send(transfers):
+        tr, rd = [], []
+        for es, sem, src, dsts in transfers:
+            code = SCRATCH[src[0]][2] == COD
+            b = (lambda v: v.bitcast(dt.uint8)) if code else (lambda v: v)
+            tr.append(RemoteDMATransfer(dst_ids=[_dst(c, topo) for c, _ in dsts], dma_engine_mask=_bits(es), remote_sem=T.sem[sem],
+                                        srcs=[b(view(src))], dsts=[b(view(x)) for _, x in dsts]))
+            rd.append(src)
+            sent[0] += len(es)
+        before("g", rd, [])
+        g.remote_dma_fused(tr, local_sem=T.sem.sent)
+
+    def spread(t, k):
+        src = ("HW%d%s" % (t, k), CO, CO + G)
+        x = ("CA%d%s" % (t, k), G * rank, G * rank + G)
+        send([(efar, "aC%d" % t, src, [(T.cores[r], x) for r in far]), (enear, "aC%d" % t, src, [(T.cores[r], x) for r in near])])
+
+    def tokens(t, k):
+        nm, a = ("XQ0", 0) if t == 0 else ("XQ12", TOK * (t - 1))
+        hx, ha = _relay(t)
+        src = (nm + k, a, a + TOK)
+        o = tb + TOK * sl
+        send([(enear[hn2:], "h%s%d" % (k, t), src, [(_helper_of(core, T, topo), (hx + k, ha, ha + TOK))]),
+              (enear[:hn2], "aT%d" % t, src, [(T.cores[r], ("TK%d%s" % (t, k), o, o + TOK)) for r in near])])
+
+    dma("y", T.CBT[:, 0:4 * G], T.cb[:], [], [("CBT", 0, 4 * G)])
+    dma("s", T.X0[:, 0:4 * TOK], T.x[:, 0:4 * TOK], [], [("X0", 0, 4 * TOK)])
+    dma("y", T.X12[:], T.x[:, 4 * TOK:12 * TOK], [], [("X12", 0, 8 * TOK)])
+    dma("s", T.WT[:], T.w[:], [], [("WT", 0, 512)])
+
+    def iota(x, pat, base, ch):
+        if SCRATCH[x[0]][2] == I32:
+            op("g", lambda e: e.iota(view(x), pat, base, ch), [], [x])
+        else:
+            op("g", lambda e: e.iota(view(x), pat, base, ch, allow_small_or_imprecise_dtypes=True), [], [x])
+
+    iota(("DV", 0, 128), [[1, 128]], 0, -1)
+    for e in range(2):
+        iota(("THR", 64 * e, 64 * e + 64), [[1, G], [1, 4]], G * own[e], 0)
+    iota(("KP", 0, 128), [[0, 8], [1, 16]], G * part, 0)
+    iota(("KO", 0, 128), [[0, 8], [1, 16]], G * rank, 0)
+    iota(("RI", 0, 128), [[0, 4], [1, 32]], 0, 0)
+    iota(("QI", 0, 1), [[0, 1]], 0, 1)
+    iota(("NV", 0, 32), [[0, 8], [-TOK, 4]], 4 * TOK, -1)
+    fill(("CBT", 4 * G, 512), 0.0)
+    fill(("ZT", 0, 704), 0.0)
+    for t in range(R):
+        qz("TK%d" % t, tb + 4 * TOK, 128, "ZT")
+    qz("HW0", 0, 128, "ZT")
+    fill(("X0", 4 * TOK, 512), 0.0)
+    qz("HW0", CO, 128, "CBT")
+    qz("XQ0", 0, 128, "X0")
+    for k in "cs":
+        tokens(0, k)
+        spread(0, k)
+    lcopy("y", "CA0", G * rank, "HW0", CO, G)
+    lcopy("s", "TK0", tb + TOK * sl, "XQ0", 0, TOK)
+    qz("XQ12", 0, 2 * TOK, "X12")
+    for t in range(1, R):
+        for k in "cs":
+            tokens(t, k)
+        lcopy("y", "TK%d" % t, tb + TOK * sl, "XQ12", TOK * (t - 1), TOK)
+    for t in range(R):
+        came = 2 * hn2 + 2 * len(efar) * len([r for r in _half(rank) if r in far])
+        for s in range(H):
+            if s != sl:
+                ext("aT%d" % t, came, [("TK%d%s" % (t, k), tb + TOK * s, tb + TOK * s + TOK) for k in "cs"])
+        for r in peers:
+            ext("aC%d" % t, 2 * (len(efar) * len(far) + len(enear) * len(near)), [("CA%d%s" % (t, k), G * r, G * r + G) for k in "cs"])
+        ext("aK%d" % t, 2 * len(efar), [("TK%d%s" % (t, k), lb, lb + 32) for k in "cs"])
+        ext("aL%d" % t, len(efar), [("LN%d" % t, 0, 2)])
+
+    fill(("NEG", 0, 128), -1e29)
+    for e in range(2):
+        for i in range(2):
+            fill(("THR", 64 * e + 2 + i, 64 * e + 64, 4), float(G * (own[e] + i)))
+    dv, ta, tc = ("DV", 0, 128), ("TA", 0, 128), ("TA", 128, 256)
+    ts(("TRT", 2, 512, 4), dv, 1.0, AL.is_ge)
+    ts(("TRT", 3, 512, 4), dv, 1.0, AL.is_ge, -1.0, AL.mult)
+    ts(ta, dv, 1.0, AL.is_ge, 128.0, AL.mult)
+    ts(tc, dv, 0.0, AL.is_equal, float(BIGW), AL.mult)
+    tt(ta, ta, tc, AL.add)
+    cp(("TRT", 0, 512, 4), ta)
+    ts(("TRT", 1, 512, 4), ta, -1.0, AL.mult)
+    fill(("TRT", 4 * TOK, 512), 0.0)
+    op("v", lambda v: v.memset(T.TRT[TOK:128, :], 0.0), [], [("TRT", 0, 512)])
+    qz("TRQ", 0, 128, "TRT")
+    ts(("RM", 0, 128), ("RI", 0, 128), 0.5, AL.is_ge)
+    ts(("NV", 32, 64), ("NV", 0, 32), 16.0, AL.add)
+    ts(("NV", 64, 96), ("NV", 32, 64), 5, AL.arith_shift_right)
+    ts(("HI", 0, 32), ("NV", 64, 96), 32.0, AL.mult)
+    tt(("LO", 0, 32), ("NV", 0, 32), ("HI", 0, 32), AL.subtract)
+    ts(("QJ", 0, 1), ("QI", 0, 1), 15, AL.bitwise_and)
+    cp(("QC", 0, 1), ("QJ", 0, 1))
+    for i in range(2):
+        ts(("KC", i, i + 1), ("QC", 0, 1), -1.0, AL.mult, float(32 - 16 * i + (4 * TOK if half else 0)), AL.add)
+    ts(("QC", 0, 1), ("QC", 0, 1), 16.0, AL.add)
+    fill(("YF", 0, 32), 0.0)
+    fill(("Y", 64, 544), 0.0)
+    for t in range(1, R + 1):
+        qz("HW%d" % t, 0, 176, "ZT")
+    for t in range(R):
+        qz("PK%d" % t, 0, 128, "ZT")
+    fill(("NEW", 64, 512), 0.0)
+    fill(("E25", 0, 2048), 0.0)
+    for b in range(4):
+        ts(("E25", 512 * b + b, 512 * b + 512, 4), dv, 0.0, AL.is_equal, 0.25, AL.mult)
+    act(("E50", 0, 2048), ("E25", 0, 2048), AF.Copy, scale=2.0)
+    qz("WQ", 0, 128, "WT")
+
+    for t in range(R):
+        tk, ca, pp, pk, hw, hn = "TK%d" % t, "CA%d" % t, "PP%d" % t, "PK%d" % t, "HW%d" % t, "HW%d" % (t + 1)
+        np_, ln, kb, kn = "NP%d" % t, "LN%d" % t, "KB%d" % t, "KN%d" % t
+        for s in range(H):
+            mm(s, tk, tb + TOK * s, ca, 0)
+        for s in range(H):
+            r = ("RB", 128 * s, 128 * s + 128)
+            scan(r, ("PS", 512 * s, 512 * s + 128), ("NEG", 0, 128), -1e29, AL.max, AL.max)
+            act(("J", 128 * s, 128 * s + 128), r, AF.Sign, bias=("RB", 128 * s + 127, 128 * s + 128), scale=-1.0, acc=("WV", s, s + 1))
+        for s in range(H):
+            ts(("OT", 128 * s, 128 * s + 128), ("THR", 0, 128), ("WV", s, s + 1), AL.is_le)
+        qz("OC", 0, 128, "OT")
+        mm(4, "TRQ", 0, "OC", 0)
+        for s in range(H):
+            o, w, j = ("NT", s, 512, 4), ("WV", s, s + 1), ("JA", 128 * (s % 2), 128 * (s % 2) + 128)
+            if s < 2:
+                ts(o, ("KP", 0, 128), w, AL.is_equal)
+            else:
+                act(j, ("KP", 0, 128), AF.Abs, bias=w, scale=-1.0)
+                act(o, j, AF.Relu, bias=1.0, scale=-1.0)
+        qz("NQ", 0, 128, "NT")
+        scan(("SC", 0, 128), ("RM", 0, 128), ("PS", 2048, 2176), 0.0, AL.mult, AL.max)
+        mk = ("SC", 31, 128, 32)
+        for i in range(2):
+            lo, cc = BIGW + 128 * i, ("CC", 4 * i, 4 * i + 4)
+            ts(cc, mk, float(lo + CAPP - 1), AL.min, float(lo), AL.max)
+            tt(("YF", 16 * i, 16 * i + 16, 5), cc, mk, AL.is_equal)
+        tt(("Y", 0, 32), ("YF", 0, 32), ("HI", 0, 32), AL.mult)
+        tt(("Y", 32, 64), ("YF", 0, 32), ("LO", 0, 32), AL.mult)
+        qz("YQ", 0, 136, "Y")
+        mm(5, "NQ", 0, "YQ", 0, True, False)
+        mm(5, "NQ", 0, "YQ", 8, False, True)
+        lp = ("PS", 2560, 2568)
+        red((np_, 0, 1), lp, AL.max)
+        ts(("XA", 0, 8), lp, (np_, 0, 1), AL.is_lt)
+        tt(("XA", 0, 8), ("XA", 0, 8), lp, AL.mult)
+        red((np_, 1, 2), ("XA", 0, 8), AL.max)
+        ts(("OP%d" % t, 0, 2), (np_, 0, 2), -1.0, AL.mult, float(4 * TOK), AL.add)
+        send([(efar, "aL%d" % t, (np_, 0, 2), [(T.cores[part], (ln, 0, 2))])])
+        pick(pp, 0, tk, tb, (lb if half == 0 else TW), "OP%d" % t, 0, 2)
+        for k in "cs":
+            send([(efar, "aK%d" % t, (pp + k, 0, 32), [(T.cores[part], (tk + k, _land(part), _land(part) + 32))])])
+        for s in range(H):
+            ts(("NO", s, 512, 4), ("KO", 0, 128), ("WV", s, s + 1), AL.is_equal)
+        qz("NOQ", 0, 128, "NO")
+        mm(6, "NOQ", 0, "YQ", 0, True, False)
+        mm(6, "NOQ", 0, "YQ", 8, False, True)
+        lo = ("PS", 3072, 3080)
+        if up:
+            ts((kb, 0, 8), lo, 0.5, AL.is_ge, float(up), AL.mult)
+            tt((kb, 0, 8), (kb, 0, 8), lo, AL.add)
+        else:
+            cp((kb, 0, 8), lo)
+        ts((kn, 0, 8), (kb, 0, 8), -1.0, AL.mult, 449.0 if half == 0 else 769.0, AL.add)
+        ts(("XA", 0, 8), (kb, 0, 8), 0.5, AL.is_ge)
+        tt((kn, 0, 8), (kn, 0, 8), ("XA", 0, 8), AL.mult)
+        if t == 0:
+            qz("E50Q", 0, 512, "E50")
+            qz("E25Q", 0, 512, "E25")
+        for b in range(4):
+            mm(7, "E50Q", 128 * b, hw, CO - 16 * b, b == 0, b == 3)
+        act(("HC", 0, 64), ("PS", 3584, 3584 + 64), AF.Copy)
+        for i in range(2):
+            ts((kb, 8 + i, 9 + i), (ln, i, i + 1), 0.5, AL.is_ge, ("KC", i, i + 1), AL.mult)
+        red(("MM", 0, 1), (kb, 0, 10), AL.max)
+        ts(("XB", 0, 10), (kb, 0, 10), ("MM", 0, 1), AL.is_lt)
+        tt(("XB", 0, 10), ("XB", 0, 10), (kb, 0, 10), AL.mult)
+        red(("MM", 2, 3), ("XB", 0, 10), AL.max)
+        ts(("TT", 0, 1), ("MM", 2, 3), 0.5, AL.is_lt, ("MM", 0, 1), AL.mult)
+        tt(("MM", 1, 2), ("TT", 0, 1), ("MM", 2, 3), AL.add)
+        ts(("OF%d" % t, 0, 3), ("MM", 0, 3), -1.0, AL.mult, float(zo), AL.add)
+        pick(pk, 0, tk, 0, TW, "OF%d" % t, 0, 3)
+        for b in range(4):
+            mm(b, "E25Q", 128 * b, pk, 0)
+        ts(("TT", 1, 2), ("MM", 0, 1), 0.5, AL.is_ge, 16.0, AL.mult)
+        ts(("OS%d" % t, 0, 1), ("TT", 1, 2), ("QC", 0, 1), AL.add)
+        for b in range(4):
+            c = 16 * b
+            act(("SS", c, c + 16), ("PS", 512 * b + 16, 512 * b + 32), AF.Copy)
+            tt(("HB", c, c + 16), ("PS", 512 * b, 512 * b + 16), ("SS", c, c + 16), AL.add)
+            tt(("NEW", b, 64, 4), ("HB", c, c + 16), ("HC", c, c + 16), AL.add)
+        qz(hw, CO + G, 128, "NEW")
+        pick(hn, CO, hw, 32, 96, "OS%d" % t, 0, 1)
+        if t + 1 < R:
+            for k in "cs":
+                spread(t + 1, k)
+            pick("CA%d" % (t + 1), G * rank, hw, 32, 96, "OS%d" % t, 0, 1)
+        else:
+            i = (hn + "c", CO, CO + G)
+            dma("y", T.oc[:, 0:4 * G], view(i).bitcast(dt.uint8), [i], [])
+            for k in range(4):
+                dma("ys"[k % 2], T.osc[4 * k:4 * k + 4, 0:G], T[hn + "s"][32 * k:32 * k + 4, CO:CO + G], [(hn + "s", CO, CO + G)], [])
+        mm(6, "WQ", 0, pk, 0)
+        act(("YO", 32 * t, 32 * t + 32, 2), ("PS", 3072, 3072 + 16), AF.Copy)
+        act(("YO", 32 * t + 1, 32 * t + 32, 2), ("PS", 3072 + 32, 3072 + 48), AF.Copy)
+        dma("y", T.y[:, 32 * t:32 * t + 32], T.YO[:, 32 * t:32 * t + 32], [("YO", 32 * t, 32 * t + 32)], [])
+        ts((kn, 8, 10), (ln, 0, 2), -1.0, AL.mult, float(769 if half == 0 else 385), AL.add)
+        ts(("IB", 0, 2), (ln, 0, 2), 0.5, AL.is_ge)
+        tt((kn, 8, 10), (kn, 8, 10), ("IB", 0, 2), AL.mult)
+        for i in range(2):
+            ts(("XB", 0, 10), (kb, 0, 10), ("MM", 2 * i, 2 * i + 1), AL.is_equal)
+            tt(("XB", 0, 10), ("XB", 0, 10), (kn, 0, 10), AL.mult)
+            red(("SN", i, i + 1), ("XB", 0, 10), AL.add)
+        ts(("ID%d" % t, 0, 2), ("SN", 0, 2), -1.0, AL.add)
+        dma("y", T.ids[:, 32 * t:32 * t + 32], T["ID%d" % t][0:16, 0:2], [("ID%d" % t, 0, 2)], [])
+
+    for q in cnt:
+        wait("g", (done[q], cnt[q]))
+    for i in range(nd[0]):
+        wait("g", ("d%d" % i, 16))
+    g.wait_ge(T.sem.sent, sent[0])

@@ -5,6 +5,7 @@ G, TOK, CAPP, R, H = 16, 96, 48, 3, 4
 TW = 544
 BIGW = 16384
 CO = 48
+BYH = 1
 
 F32, BF, I32, U16, COD, PLN = "float32", "bfloat16", "int32", "uint16", "float8_e4m3fn_x4", "uint8"
 SCRATCH = {"PS": ("psum", [128, 4096], F32)}
@@ -44,7 +45,7 @@ for _t in range(R):
     _buf("OP%d" % _t, 2, U16)
     _buf("OF%d" % _t, 4, U16)
     _buf("OS%d" % _t, 2, U16)
-    SEMAPHORES += ["aC%d" % _t, "aT%d" % _t, "aL%d" % _t, "aK%d" % _t, "hc%d" % _t, "hs%d" % _t]
+    SEMAPHORES += ["aC%d" % _t, "aT%d" % _t, "aL%d" % _t, "aK%d" % _t, "hc%d" % _t, "hs%d" % _t, "gc%d" % _t, "gs%d" % _t]
 for _t in range(R + 1):
     _mx("HW%d" % _t, 192)
 SEMAPHORES += ["d%d" % _i for _i in range(30)]
@@ -79,6 +80,12 @@ def _relay(t):
     return ("HX0", 0) if t == 0 else ("HX12", TOK * (t - 1))
 
 
+def _far(rank, T, topo):
+    n = len(T.cores)
+    order = [(rank + i) % n for i in range(1, n)]
+    return [r for r in order if topo.chip(T.cores[r]) != topo.chip(T.cores[rank])]
+
+
 def _near_engines(a, b, far, topo):
     return [e for e in topo.engines(a, b) if e not in topo.engines(a, far)]
 
@@ -87,11 +94,11 @@ def _helper(g, core, rank, T, topo):
     me = T.cores[rank]
     far = [r for r in _half(rank) if topo.chip(T.cores[r]) != topo.chip(me)]
     es = topo.engines(core, T.cores[far[0]])
-    came = len(_near_engines(me, core, T.cores[far[0]], topo)) // 2
+    near = _near_engines(me, core, T.cores[far[0]], topo)
     n = 0
     for t in range(R):
         for k in "cs":
-            g.wait_ge(T.sem["h%s%d" % (k, t)], came)
+            g.wait_ge(T.sem["h%s%d" % (k, t)], len(near) if t == 0 else len(near) // 2)
             dsts = []
             for r in far:
                 o = _base(r) + TOK * (rank % H)
@@ -103,6 +110,17 @@ def _helper(g, core, rank, T, topo):
             g.remote_dma_fused([RemoteDMATransfer(dst_ids=[_dst(T.cores[r], topo) for r in far], dma_engine_mask=_bits(es),
                                                   remote_sem=T.sem["aT%d" % t], srcs=[src], dsts=dsts)], local_sem=T.sem.sent)
             n += len(es)
+    last = _far(rank, T, topo)[-BYH:]
+    mate = [r for r in range(len(T.cores)) if r != rank and topo.chip(T.cores[r]) == topo.chip(me)]
+    en = _near_engines(core, T.cores[mate[0]], T.cores[far[0]], topo)
+    for t in range(1, R):
+        for k in "cs":
+            g.wait_ge(T.sem["g%s%d" % (k, t)], len(near))
+            v = T["CA%d%s" % (t, k)][:, G * rank:G * rank + G]
+            v = v.bitcast(dt.uint8) if k == "c" else v
+            g.remote_dma_fused([RemoteDMATransfer(dst_ids=[_dst(T.cores[r], topo) for r in rs], dma_engine_mask=_bits(e), remote_sem=T.sem["aC%d" % t],
+                                                  srcs=[v], dsts=[v] * len(rs)) for e, rs in ((es, last), (en, mate))], local_sem=T.sem.sent)
+            n += len(es) + len(en)
     g.wait_ge(T.sem.sent, n)
 
 
@@ -240,7 +258,7 @@ def rank_program(g, core, T, topo):
 
     peers = [r for r in range(len(T.cores)) if r != rank]
     near = [r for r in peers if topo.chip(T.cores[r]) == topo.chip(core)]
-    far = [r for r in peers if r not in near]
+    far = _far(rank, T, topo)
     efar = topo.engines(core, T.cores[far[0]])
     enear = _near_engines(core, T.cores[near[0]], T.cores[far[0]], topo)
     hn2 = len(enear) // 2
@@ -258,18 +276,29 @@ def rank_program(g, core, T, topo):
         before("g", rd, [])
         g.remote_dma_fused(tr, local_sem=T.sem.sent)
 
-    def spread(t, k):
+    def spread(t, k, es):
         src = ("HW%d%s" % (t, k), CO, CO + G)
         x = ("CA%d%s" % (t, k), G * rank, G * rank + G)
-        send([(efar, "aC%d" % t, src, [(T.cores[r], x) for r in far]), (enear, "aC%d" % t, src, [(T.cores[r], x) for r in near])])
+        tr = []
+        if es[0]:
+            tr.append((es[0], "aC%d" % t, src, [(T.cores[r], x) for r in far[:len(far) if t == 0 else -BYH]]))
+        if len(es) > 1 and t == 0:
+            tr.append((es[1], "aC%d" % t, src, [(T.cores[r], x) for r in near]))
+        elif len(es) > 1:
+            tr.append((es[1], "g%s%d" % (k, t), src, [(_helper_of(core, T, topo), x)]))
+        send(tr)
 
-    def tokens(t, k):
+    def tokens(t, k, es):
         nm, a = ("XQ0", 0) if t == 0 else ("XQ12", TOK * (t - 1))
         hx, ha = _relay(t)
         src = (nm + k, a, a + TOK)
         o = tb + TOK * sl
-        send([(enear[hn2:], "h%s%d" % (k, t), src, [(_helper_of(core, T, topo), (hx + k, ha, ha + TOK))]),
-              (enear[:hn2], "aT%d" % t, src, [(T.cores[r], ("TK%d%s" % (t, k), o, o + TOK)) for r in near])])
+        tr = []
+        if es[0]:
+            tr.append((es[0], "h%s%d" % (k, t), src, [(_helper_of(core, T, topo), (hx + k, ha, ha + TOK))]))
+        if es[1]:
+            tr.append((es[1], "aT%d" % t, src, [(T.cores[r], ("TK%d%s" % (t, k), o, o + TOK)) for r in near]))
+        send(tr)
 
     dma("y", T.CBT[:, 0:4 * G], T.cb[:], [], [("CBT", 0, 4 * G)])
     dma("s", T.X0[:, 0:4 * TOK], T.x[:, 0:4 * TOK], [], [("X0", 0, 4 * TOK)])
@@ -299,17 +328,21 @@ def rank_program(g, core, T, topo):
     qz("HW0", CO, 128, "CBT")
     qz("XQ0", 0, 128, "X0")
     for k in "cs":
-        tokens(0, k)
-        spread(0, k)
+        spread(0, k, [efar])
+        tokens(0, k, [enear, []])
+    for k in "cs":
+        spread(0, k, [[], enear])
+    for k in "cs":
+        tokens(0, k, [[], enear])
     lcopy("y", "CA0", G * rank, "HW0", CO, G)
     lcopy("s", "TK0", tb + TOK * sl, "XQ0", 0, TOK)
     qz("XQ12", 0, 2 * TOK, "X12")
     for t in range(1, R):
         for k in "cs":
-            tokens(t, k)
+            tokens(t, k, [enear[hn2:], enear[:hn2]])
         lcopy("y", "TK%d" % t, tb + TOK * sl, "XQ12", TOK * (t - 1), TOK)
     for t in range(R):
-        came = 2 * hn2 + 2 * len(efar) * len([r for r in _half(rank) if r in far])
+        came = 2 * (len(enear) if t == 0 else hn2) + 2 * len(efar) * len([r for r in _half(rank) if r in far])
         for s in range(H):
             if s != sl:
                 ext("aT%d" % t, came, [("TK%d%s" % (t, k), tb + TOK * s, tb + TOK * s + TOK) for k in "cs"])
@@ -318,6 +351,10 @@ def rank_program(g, core, T, topo):
         ext("aK%d" % t, 2 * len(efar), [("TK%d%s" % (t, k), lb, lb + 32) for k in "cs"])
         ext("aL%d" % t, len(efar), [("LN%d" % t, 0, 2)])
 
+    for b in range(4):
+        act(("E25", 512 * b, 512 * b + 512), ("ZT", 0, 512), AF.Copy)
+    act(("Y", 64, 544), ("ZT", 0, 480), AF.Copy)
+    act(("NEW", 64, 512), ("ZT", 0, 448), AF.Copy)
     fill(("NEG", 0, 128), -1e29)
     for e in range(2):
         for i in range(2):
@@ -344,17 +381,12 @@ def rank_program(g, core, T, topo):
         ts(("KC", i, i + 1), ("QC", 0, 1), -1.0, AL.mult, float(32 - 16 * i + (4 * TOK if half else 0)), AL.add)
     ts(("QC", 0, 1), ("QC", 0, 1), 16.0, AL.add)
     fill(("YF", 0, 32), 0.0)
-    fill(("Y", 64, 544), 0.0)
-    for t in range(1, R + 1):
-        qz("HW%d" % t, 0, 176, "ZT")
-    for t in range(R):
-        qz("PK%d" % t, 0, 128, "ZT")
-    fill(("NEW", 64, 512), 0.0)
-    fill(("E25", 0, 2048), 0.0)
     for b in range(4):
         ts(("E25", 512 * b + b, 512 * b + 512, 4), dv, 0.0, AL.is_equal, 0.25, AL.mult)
     act(("E50", 0, 2048), ("E25", 0, 2048), AF.Copy, scale=2.0)
-    qz("WQ", 0, 128, "WT")
+    qz("HW1", 0, 176, "ZT")
+    qz("PK0", 0, 128, "ZT")
+    qz("E25Q", 0, 512, "E25")
 
     for t in range(R):
         tk, ca, pp, pk, hw, hn = "TK%d" % t, "CA%d" % t, "PP%d" % t, "PK%d" % t, "HW%d" % t, "HW%d" % (t + 1)
@@ -371,7 +403,7 @@ def rank_program(g, core, T, topo):
         mm(4, "TRQ", 0, "OC", 0)
         for s in range(H):
             o, w, j = ("NT", s, 512, 4), ("WV", s, s + 1), ("JA", 128 * (s % 2), 128 * (s % 2) + 128)
-            if s < 2:
+            if s < 3:
                 ts(o, ("KP", 0, 128), w, AL.is_equal)
             else:
                 act(j, ("KP", 0, 128), AF.Abs, bias=w, scale=-1.0)
@@ -414,7 +446,6 @@ def rank_program(g, core, T, topo):
         tt((kn, 0, 8), (kn, 0, 8), ("XA", 0, 8), AL.mult)
         if t == 0:
             qz("E50Q", 0, 512, "E50")
-            qz("E25Q", 0, 512, "E25")
         for b in range(4):
             mm(7, "E50Q", 128 * b, hw, CO - 16 * b, b == 0, b == 3)
         act(("HC", 0, 64), ("PS", 3584, 3584 + 64), AF.Copy)
@@ -432,6 +463,9 @@ def rank_program(g, core, T, topo):
             mm(b, "E25Q", 128 * b, pk, 0)
         ts(("TT", 1, 2), ("MM", 0, 1), 0.5, AL.is_ge, 16.0, AL.mult)
         ts(("OS%d" % t, 0, 1), ("TT", 1, 2), ("QC", 0, 1), AL.add)
+        ts((kn, 8, 10), (ln, 0, 2), -1.0, AL.mult, float(769 if half == 0 else 385), AL.add)
+        ts(("IB", 0, 2), (ln, 0, 2), 0.5, AL.is_ge)
+        tt((kn, 8, 10), (kn, 8, 10), ("IB", 0, 2), AL.mult)
         for b in range(4):
             c = 16 * b
             act(("SS", c, c + 16), ("PS", 512 * b + 16, 512 * b + 32), AF.Copy)
@@ -441,20 +475,22 @@ def rank_program(g, core, T, topo):
         pick(hn, CO, hw, 32, 96, "OS%d" % t, 0, 1)
         if t + 1 < R:
             for k in "cs":
-                spread(t + 1, k)
+                spread(t + 1, k, [efar, enear])
             pick("CA%d" % (t + 1), G * rank, hw, 32, 96, "OS%d" % t, 0, 1)
         else:
             i = (hn + "c", CO, CO + G)
             dma("y", T.oc[:, 0:4 * G], view(i).bitcast(dt.uint8), [i], [])
             for k in range(4):
                 dma("ys"[k % 2], T.osc[4 * k:4 * k + 4, 0:G], T[hn + "s"][32 * k:32 * k + 4, CO:CO + G], [(hn + "s", CO, CO + G)], [])
+        if t == 0:
+            qz("WQ", 0, 128, "WT")
+        if t + 1 < R:
+            qz("PK%d" % (t + 1), 0, 128, "ZT")
+            qz("HW%d" % (t + 2), 0, 176, "ZT")
         mm(6, "WQ", 0, pk, 0)
         act(("YO", 32 * t, 32 * t + 32, 2), ("PS", 3072, 3072 + 16), AF.Copy)
         act(("YO", 32 * t + 1, 32 * t + 32, 2), ("PS", 3072 + 32, 3072 + 48), AF.Copy)
         dma("y", T.y[:, 32 * t:32 * t + 32], T.YO[:, 32 * t:32 * t + 32], [("YO", 32 * t, 32 * t + 32)], [])
-        ts((kn, 8, 10), (ln, 0, 2), -1.0, AL.mult, float(769 if half == 0 else 385), AL.add)
-        ts(("IB", 0, 2), (ln, 0, 2), 0.5, AL.is_ge)
-        tt((kn, 8, 10), (kn, 8, 10), ("IB", 0, 2), AL.mult)
         for i in range(2):
             ts(("XB", 0, 10), (kb, 0, 10), ("MM", 2 * i, 2 * i + 1), AL.is_equal)
             tt(("XB", 0, 10), ("XB", 0, 10), (kn, 0, 10), AL.mult)

@@ -5,7 +5,7 @@ G, TOK, CAPP, R, H = 16, 96, 48, 3, 4
 TW = 544
 BIGW = 16384
 CO = 48
-BYH = 1
+BY0, BYH = {"c": 0, "s": 2}, {"c": 2, "s": 1}
 
 F32, BF, I32, U16, COD, PLN = "float32", "bfloat16", "int32", "uint16", "float8_e4m3fn_x4", "uint8"
 SCRATCH = {"PS": ("psum", [128, 4096], F32)}
@@ -21,33 +21,32 @@ def _mx(name, n):
     _buf(name + "s", n, PLN)
 
 
-for _n, _w in (("CBT", 512), ("X0", 512), ("X12", 768), ("WT", 512), ("ZT", 704), ("TRT", 512), ("E25", 2048), ("E50", 2048), ("THR", 128), ("KP", 128),
+for _n, _w in (("CBT", 512), ("X0", 512), ("X12", 768), ("WT", 512), ("ZT", 704), ("TRT", 512), ("E25", 2048), ("THR", 128), ("KP", 128),
                ("KO", 128), ("HI", 32), ("LO", 32), ("OT", 512), ("NT", 512), ("NO", 512), ("YF", 32), ("Y", 544), ("NEW", 512), ("J", 512), ("JA", 256)):
     _buf(_n, _w, BF)
-for _n, _w in (("RM", 128), ("NEG", 128), ("DV", 128), ("TA", 256), ("QC", 1), ("KC", 2), ("RB", 512), ("WV", 4), ("SC", 128), ("CC", 8), ("XA", 16),
-               ("XB", 16), ("MM", 4), ("TT", 4), ("SS", 64), ("HB", 64), ("HC", 64), ("YO", 96), ("SN", 2), ("IB", 2)):
+for _n, _w in (("RM", 128), ("NEG", 128), ("DV", 128), ("TA", 256), ("QC", 1), ("KC", 2), ("RB", 512), ("WV", 4), ("SC", 128), ("CC", 8), ("XA", 8),
+               ("OW", 2), ("LK", 2), ("MM", 4), ("TT", 4), ("SS", 64), ("HB", 64), ("WN", 128), ("HC", 64), ("BQ", 4), ("YO", 96)):
     _buf(_n, _w, F32)
-for _n, _w in (("QI", 1), ("QJ", 1), ("NV", 96), ("RI", 128)):
+for _n, _w in (("QI", 1), ("QJ", 1), ("NV", 96), ("RI", 128), ("WI", 4), ("WJ", 4)):
     _buf(_n, _w, I32)
-for _n, _w in (("XQ0", 128), ("XQ12", 192), ("WQ", 128), ("TRQ", 128), ("E25Q", 512), ("E50Q", 512), ("OC", 128), ("NQ", 128), ("NOQ", 128), ("YQ", 136),
+for _n, _w in (("XQ0", 128), ("XQ12", 192), ("WQ", 128), ("TRQ", 128), ("E25Q", 512), ("OC", 128), ("NQ", 128), ("NOQ", 128), ("YQ", 136),
                ("HX0", 96), ("HX12", 192)):
     _mx(_n, _w)
 for _t in range(R):
     _mx("TK%d" % _t, TW)
     _mx("CA%d" % _t, 128)
     _mx("PP%d" % _t, 32)
-    _mx("PK%d" % _t, 128)
+    _mx("PK%d" % _t, 144)
     _buf("NP%d" % _t, 2, F32)
     _buf("LN%d" % _t, 2, F32)
-    _buf("KB%d" % _t, 12, F32)
-    _buf("KN%d" % _t, 12, F32)
+    _buf("KB%d" % _t, 8, F32)
     _buf("ID%d" % _t, 2, F32)
     _buf("OP%d" % _t, 2, U16)
     _buf("OF%d" % _t, 4, U16)
-    _buf("OS%d" % _t, 2, U16)
+    _buf("OS%d" % _t, 4, U16)
     SEMAPHORES += ["aC%d" % _t, "aT%d" % _t, "aL%d" % _t, "aK%d" % _t, "hc%d" % _t, "hs%d" % _t, "gc%d" % _t, "gs%d" % _t]
 for _t in range(R + 1):
-    _mx("HW%d" % _t, 192)
+    _mx("HW%d" % _t, 176)
 SEMAPHORES += ["d%d" % _i for _i in range(30)]
 
 
@@ -55,8 +54,8 @@ def _bits(es):
     return sum(1 << e for e in es)
 
 
-def _helper_of(core, T, topo):
-    return [c for c in topo.cores_of(core) if T.rank_of(c) is None and topo.die(c) == topo.die(core)][0]
+def _helper_of(core, T, topo, i=0):
+    return [c for c in topo.cores_of(core) if T.rank_of(c) is None and topo.die(c) == topo.die(core)][i]
 
 
 def _half(r):
@@ -110,11 +109,11 @@ def _helper(g, core, rank, T, topo):
             g.remote_dma_fused([RemoteDMATransfer(dst_ids=[_dst(T.cores[r], topo) for r in far], dma_engine_mask=_bits(es),
                                                   remote_sem=T.sem["aT%d" % t], srcs=[src], dsts=dsts)], local_sem=T.sem.sent)
             n += len(es)
-    last = _far(rank, T, topo)[-BYH:]
     mate = [r for r in range(len(T.cores)) if r != rank and topo.chip(T.cores[r]) == topo.chip(me)]
     en = _near_engines(core, T.cores[mate[0]], T.cores[far[0]], topo)
     for t in range(1, R):
         for k in "cs":
+            last = _far(rank, T, topo)[-BYH[k]:]
             g.wait_ge(T.sem["g%s%d" % (k, t)], len(near))
             v = T["CA%d%s" % (t, k)][:, G * rank:G * rank + G]
             v = v.bitcast(dt.uint8) if k == "c" else v
@@ -124,12 +123,24 @@ def _helper(g, core, rank, T, topo):
     g.wait_ge(T.sem.sent, n)
 
 
+def _first(g, core, rank, T, topo):
+    last = _far(rank, T, topo)[-BY0["s"]:]
+    es = topo.engines(core, T.cores[last[0]])
+    g.wait_ge(T.sem.gs0, len(_near_engines(T.cores[rank], core, T.cores[last[0]], topo)))
+    v = T.CA0s[:, G * rank:G * rank + G]
+    g.remote_dma_fused([RemoteDMATransfer(dst_ids=[_dst(T.cores[r], topo) for r in last], dma_engine_mask=_bits(es), remote_sem=T.sem.aC0,
+                                          srcs=[v], dsts=[v] * len(last))], local_sem=T.sem.sent)
+    g.wait_ge(T.sem.sent, len(es))
+
+
 def rank_program(g, core, T, topo):
     rank = T.rank_of(core)
     if rank is None:
         for r in range(len(T.cores)):
             if _helper_of(T.cores[r], T, topo) == core:
                 _helper(g, core, r, T, topo)
+            if _helper_of(T.cores[r], T, topo, 1) == core:
+                _first(g, core, r, T, topo)
         return
     AL, AF, AX = AluOpType, ActivationFunctionType, AxisListType.X
     half, sl = rank // H, rank % H
@@ -138,6 +149,7 @@ def rank_program(g, core, T, topo):
     tb, lb = _base(rank), _land(rank)
     zo = tb + 4 * TOK + (64 if half == 0 else 0)
     up = 64 if half == 0 else 0
+    on1, ln1 = (H * TOK + 1, 2 * H * TOK + 1) if half == 0 else (2 * H * TOK + 1, H * TOK + 1)
     eng = {"v": g.vector, "s": g.scalar, "p": g.tensor, "g": g, "y": g.sync}
     done = {"v": "vd", "s": "sd", "p": "pd", "g": "gd"}
     cnt, seen, log, nd = {}, {}, {}, [0]
@@ -251,6 +263,12 @@ def rank_program(g, core, T, topo):
                 vi, vo = vi.bitcast(dt.uint8), vo.bitcast(dt.uint8)
             dma(q, vo, vi, [i], [o])
 
+    def iota(x, pat, base, ch):
+        if SCRATCH[x[0]][2] == I32:
+            op("g", lambda e: e.iota(view(x), pat, base, ch), [], [x])
+        else:
+            op("g", lambda e: e.iota(view(x), pat, base, ch, allow_small_or_imprecise_dtypes=True), [], [x])
+
     def ext(sem, val, xs):
         for x in xs:
             nm, cs = cols(x)
@@ -262,6 +280,7 @@ def rank_program(g, core, T, topo):
     efar = topo.engines(core, T.cores[far[0]])
     enear = _near_engines(core, T.cores[near[0]], T.cores[far[0]], topo)
     hn2 = len(enear) // 2
+    h0, h1 = _helper_of(core, T, topo), _helper_of(core, T, topo, 1)
     sent = [0]
 
     def send(transfers):
@@ -276,16 +295,15 @@ def rank_program(g, core, T, topo):
         before("g", rd, [])
         g.remote_dma_fused(tr, local_sem=T.sem.sent)
 
-    def spread(t, k, es):
+    def spread(t, k, es, to):
         src = ("HW%d%s" % (t, k), CO, CO + G)
         x = ("CA%d%s" % (t, k), G * rank, G * rank + G)
+        direct = len(far) - (BY0[k] if t == 0 else BYH[k])
         tr = []
         if es[0]:
-            tr.append((es[0], "aC%d" % t, src, [(T.cores[r], x) for r in far[:len(far) if t == 0 else -BYH]]))
-        if len(es) > 1 and t == 0:
-            tr.append((es[1], "aC%d" % t, src, [(T.cores[r], x) for r in near]))
-        elif len(es) > 1:
-            tr.append((es[1], "g%s%d" % (k, t), src, [(_helper_of(core, T, topo), x)]))
+            tr.append((es[0], "aC%d" % t, src, [(T.cores[r], x) for r in far[:direct]]))
+        if es[1]:
+            tr.append((es[1], "aC%d" % t if to == "mate" else "g%s%d" % (k, t), src, [(T.cores[near[0]] if to == "mate" else to, x)]))
         send(tr)
 
     def tokens(t, k, es):
@@ -295,7 +313,7 @@ def rank_program(g, core, T, topo):
         o = tb + TOK * sl
         tr = []
         if es[0]:
-            tr.append((es[0], "h%s%d" % (k, t), src, [(_helper_of(core, T, topo), (hx + k, ha, ha + TOK))]))
+            tr.append((es[0], "h%s%d" % (k, t), src, [(h0, (hx + k, ha, ha + TOK))]))
         if es[1]:
             tr.append((es[1], "aT%d" % t, src, [(T.cores[r], ("TK%d%s" % (t, k), o, o + TOK)) for r in near]))
         send(tr)
@@ -304,13 +322,6 @@ def rank_program(g, core, T, topo):
     dma("s", T.X0[:, 0:4 * TOK], T.x[:, 0:4 * TOK], [], [("X0", 0, 4 * TOK)])
     dma("y", T.X12[:], T.x[:, 4 * TOK:12 * TOK], [], [("X12", 0, 8 * TOK)])
     dma("s", T.WT[:], T.w[:], [], [("WT", 0, 512)])
-
-    def iota(x, pat, base, ch):
-        if SCRATCH[x[0]][2] == I32:
-            op("g", lambda e: e.iota(view(x), pat, base, ch), [], [x])
-        else:
-            op("g", lambda e: e.iota(view(x), pat, base, ch, allow_small_or_imprecise_dtypes=True), [], [x])
-
     iota(("DV", 0, 128), [[1, 128]], 0, -1)
     for e in range(2):
         iota(("THR", 64 * e, 64 * e + 64), [[1, G], [1, 4]], G * own[e], 0)
@@ -327,11 +338,12 @@ def rank_program(g, core, T, topo):
     fill(("X0", 4 * TOK, 512), 0.0)
     qz("HW0", CO, 128, "CBT")
     qz("XQ0", 0, 128, "X0")
+    spread(0, "c", [efar, []], None)
+    tokens(0, "c", [enear, []])
+    spread(0, "s", [efar, enear], h1)
+    tokens(0, "s", [enear, []])
     for k in "cs":
-        spread(0, k, [efar])
-        tokens(0, k, [enear, []])
-    for k in "cs":
-        spread(0, k, [[], enear])
+        spread(0, k, [[], enear], "mate")
     for k in "cs":
         tokens(0, k, [[], enear])
     lcopy("y", "CA0", G * rank, "HW0", CO, G)
@@ -351,46 +363,46 @@ def rank_program(g, core, T, topo):
         ext("aK%d" % t, 2 * len(efar), [("TK%d%s" % (t, k), lb, lb + 32) for k in "cs"])
         ext("aL%d" % t, len(efar), [("LN%d" % t, 0, 2)])
 
+    dv, ta, tc = ("DV", 0, 128), ("TA", 0, 128), ("TA", 128, 256)
     for b in range(4):
         act(("E25", 512 * b, 512 * b + 512), ("ZT", 0, 512), AF.Copy)
-    act(("Y", 64, 544), ("ZT", 0, 480), AF.Copy)
-    act(("NEW", 64, 512), ("ZT", 0, 448), AF.Copy)
-    fill(("NEG", 0, 128), -1e29)
+    act(("NEG", 0, 128), ("ZT", 0, 128), AF.Identity, bias=-1e29)
+    act(("YF", 0, 32), ("ZT", 0, 32), AF.Copy)
     for e in range(2):
         for i in range(2):
-            fill(("THR", 64 * e + 2 + i, 64 * e + 64, 4), float(G * (own[e] + i)))
-    dv, ta, tc = ("DV", 0, 128), ("TA", 0, 128), ("TA", 128, 256)
-    ts(("TRT", 2, 512, 4), dv, 1.0, AL.is_ge)
-    ts(("TRT", 3, 512, 4), dv, 1.0, AL.is_ge, -1.0, AL.mult)
+            iota(("THR", 64 * e + 2 + i, 64 * e + 64, 4), [[0, G]], G * (own[e] + i), 0)
     ts(ta, dv, 1.0, AL.is_ge, 128.0, AL.mult)
     ts(tc, dv, 0.0, AL.is_equal, float(BIGW), AL.mult)
+    ts(("TRT", 2, 512, 4), dv, 1.0, AL.is_ge)
     tt(ta, ta, tc, AL.add)
-    cp(("TRT", 0, 512, 4), ta)
-    ts(("TRT", 1, 512, 4), ta, -1.0, AL.mult)
+    act(("TRT", 3, 512, 4), ("TRT", 2, 512, 4), AF.Copy, scale=-1.0)
+    act(("TRT", 0, 512, 4), ta, AF.Copy)
+    act(("TRT", 1, 512, 4), ta, AF.Copy, scale=-1.0)
+    for b in range(4):
+        ts(("E25", 512 * b + b, 512 * b + 512, 4), dv, 0.0, AL.is_equal, 0.25, AL.mult)
+    ts(("QJ", 0, 1), ("QI", 0, 1), 15, AL.bitwise_and)
+    cp(("QC", 0, 1), ("QJ", 0, 1))
+    ts(("RM", 0, 128), ("RI", 0, 128), 0.5, AL.is_ge)
     fill(("TRT", 4 * TOK, 512), 0.0)
     op("v", lambda v: v.memset(T.TRT[TOK:128, :], 0.0), [], [("TRT", 0, 512)])
     qz("TRQ", 0, 128, "TRT")
-    ts(("RM", 0, 128), ("RI", 0, 128), 0.5, AL.is_ge)
     ts(("NV", 32, 64), ("NV", 0, 32), 16.0, AL.add)
     ts(("NV", 64, 96), ("NV", 32, 64), 5, AL.arith_shift_right)
     ts(("HI", 0, 32), ("NV", 64, 96), 32.0, AL.mult)
     tt(("LO", 0, 32), ("NV", 0, 32), ("HI", 0, 32), AL.subtract)
-    ts(("QJ", 0, 1), ("QI", 0, 1), 15, AL.bitwise_and)
-    cp(("QC", 0, 1), ("QJ", 0, 1))
     for i in range(2):
-        ts(("KC", i, i + 1), ("QC", 0, 1), -1.0, AL.mult, float(32 - 16 * i + (4 * TOK if half else 0)), AL.add)
-    ts(("QC", 0, 1), ("QC", 0, 1), 16.0, AL.add)
-    fill(("YF", 0, 32), 0.0)
+        act(("KC", i, i + 1), ("QC", 0, 1), AF.Identity, bias=float((32 - 16 * i + (4 * TOK if half else 0)) * 1024 + ln1), scale=-1024.0)
+    act(("Y", 64, 544), ("ZT", 0, 480), AF.Copy)
     for b in range(4):
-        ts(("E25", 512 * b + b, 512 * b + 512, 4), dv, 0.0, AL.is_equal, 0.25, AL.mult)
-    act(("E50", 0, 2048), ("E25", 0, 2048), AF.Copy, scale=2.0)
-    qz("HW1", 0, 176, "ZT")
-    qz("PK0", 0, 128, "ZT")
+        act(("BQ", b, b + 1), ("QC", 0, 1), AF.Identity, bias=float(16 * b))
+        act(("WN", 64 + 16 * b, 80 + 16 * b), ("CBT", b, 64, 4), AF.Copy)
+    qz("HW1", 0, 128, "ZT")
+    qz("PK0", 0, 144, "ZT")
     qz("E25Q", 0, 512, "E25")
 
     for t in range(R):
         tk, ca, pp, pk, hw, hn = "TK%d" % t, "CA%d" % t, "PP%d" % t, "PK%d" % t, "HW%d" % t, "HW%d" % (t + 1)
-        np_, ln, kb, kn = "NP%d" % t, "LN%d" % t, "KB%d" % t, "KN%d" % t
+        np_, ln, kb = "NP%d" % t, "LN%d" % t, "KB%d" % t
         for s in range(H):
             mm(s, tk, tb + TOK * s, ca, 0)
         for s in range(H):
@@ -408,6 +420,8 @@ def rank_program(g, core, T, topo):
             else:
                 act(j, ("KP", 0, 128), AF.Abs, bias=w, scale=-1.0)
                 act(o, j, AF.Relu, bias=1.0, scale=-1.0)
+        if t == 0:
+            act(("NEW", 64, 512), ("ZT", 0, 448), AF.Copy)
         qz("NQ", 0, 128, "NT")
         scan(("SC", 0, 128), ("RM", 0, 128), ("PS", 2048, 2176), 0.0, AL.mult, AL.max)
         mk = ("SC", 31, 128, 32)
@@ -436,47 +450,52 @@ def rank_program(g, core, T, topo):
         mm(6, "NOQ", 0, "YQ", 0, True, False)
         mm(6, "NOQ", 0, "YQ", 8, False, True)
         lo = ("PS", 3072, 3080)
-        if up:
-            ts((kb, 0, 8), lo, 0.5, AL.is_ge, float(up), AL.mult)
-            tt((kb, 0, 8), (kb, 0, 8), lo, AL.add)
-        else:
-            cp((kb, 0, 8), lo)
-        ts((kn, 0, 8), (kb, 0, 8), -1.0, AL.mult, 449.0 if half == 0 else 769.0, AL.add)
-        ts(("XA", 0, 8), (kb, 0, 8), 0.5, AL.is_ge)
-        tt((kn, 0, 8), (kn, 0, 8), ("XA", 0, 8), AL.mult)
-        if t == 0:
-            qz("E50Q", 0, 512, "E50")
+        ts(("XA", 0, 8), lo, 0.5, AL.is_ge, float(1024 * up + on1), AL.mult)
+        ts((kb, 0, 8), lo, 1023.0, AL.mult)
+        tt((kb, 0, 8), (kb, 0, 8), ("XA", 0, 8), AL.add)
+        o1, o2, l1, l2 = ("OW", 0, 1), ("OW", 1, 2), ("LK", 0, 1), ("LK", 1, 2)
+        red(o1, (kb, 0, 8), AL.max)
+        ts(("XA", 0, 8), (kb, 0, 8), o1, AL.is_lt)
+        tt(("XA", 0, 8), ("XA", 0, 8), (kb, 0, 8), AL.mult)
+        red(o2, ("XA", 0, 8), AL.max)
         for b in range(4):
-            mm(7, "E50Q", 128 * b, hw, CO - 16 * b, b == 0, b == 3)
-        act(("HC", 0, 64), ("PS", 3584, 3584 + 64), AF.Copy)
+            mm(7, "E25Q", 128 * b, hw, CO - 16 * b, b == 0, b == 3)
+        act(("WN", 0, 64), ("PS", 3584, 3584 + 64), AF.Copy, scale=2.0)
         for i in range(2):
-            ts((kb, 8 + i, 9 + i), (ln, i, i + 1), 0.5, AL.is_ge, ("KC", i, i + 1), AL.mult)
-        red(("MM", 0, 1), (kb, 0, 10), AL.max)
-        ts(("XB", 0, 10), (kb, 0, 10), ("MM", 0, 1), AL.is_lt)
-        tt(("XB", 0, 10), ("XB", 0, 10), (kb, 0, 10), AL.mult)
-        red(("MM", 2, 3), ("XB", 0, 10), AL.max)
+            ts(("LK", i, i + 1), (ln, i, i + 1), 0.5, AL.is_ge, ("KC", i, i + 1), AL.mult)
+        tt(("LK", 0, 2), ("LK", 0, 2), (ln, 0, 2), AL.subtract)
+        ts(("TT", 2, 3), l1, o1, AL.min, o2, AL.max)
+        ts(("MM", 0, 1), l1, o1, AL.max)
+        ts(("MM", 2, 3), l2, ("TT", 2, 3), AL.max)
         ts(("TT", 0, 1), ("MM", 2, 3), 0.5, AL.is_lt, ("MM", 0, 1), AL.mult)
         tt(("MM", 1, 2), ("TT", 0, 1), ("MM", 2, 3), AL.add)
-        ts(("OF%d" % t, 0, 3), ("MM", 0, 3), -1.0, AL.mult, float(zo), AL.add)
+        ts(("OF%d" % t, 0, 3), ("MM", 0, 3), -1.0 / 1024, AL.mult, zo + 0.375, AL.add)
         pick(pk, 0, tk, 0, TW, "OF%d" % t, 0, 3)
-        for b in range(4):
+        for b in range(3):
             mm(b, "E25Q", 128 * b, pk, 0)
-        ts(("TT", 1, 2), ("MM", 0, 1), 0.5, AL.is_ge, 16.0, AL.mult)
-        ts(("OS%d" % t, 0, 1), ("TT", 1, 2), ("QC", 0, 1), AL.add)
-        ts((kn, 8, 10), (ln, 0, 2), -1.0, AL.mult, float(769 if half == 0 else 385), AL.add)
-        ts(("IB", 0, 2), (ln, 0, 2), 0.5, AL.is_ge)
-        tt((kn, 8, 10), (kn, 8, 10), ("IB", 0, 2), AL.mult)
+        mm(3, "E25Q", 384, pk, 16, True, False)
+        mm(3, "E25Q", 384, pk, 0, False, True)
+        ts(("TT", 1, 2), ("MM", 0, 1), 0.5, AL.is_lt, 64.0, AL.mult)
+        ts(("OS%d" % t, 0, 4), ("BQ", 0, 4), ("TT", 1, 2), AL.add)
+        w, o, h = ("WN", 0, 128), ("OS%d" % t, 0, 4), ("HC", 0, 64)
+        op("s", lambda q, w=w, o=o, h=h: q.activation(view(h), view(w).indirect(view(o)), AF.Copy), [w, o], [h])
+        cp(("WI", 0, 3), ("MM", 0, 3))
+        ts(("WJ", 0, 3), ("WI", 0, 3), 1023, AL.bitwise_and)
+        ts(("ID%d" % t, 0, 2), ("WJ", 0, 3, 2), -1.0, AL.add)
         for b in range(4):
-            c = 16 * b
-            act(("SS", c, c + 16), ("PS", 512 * b + 16, 512 * b + 32), AF.Copy)
-            tt(("HB", c, c + 16), ("PS", 512 * b, 512 * b + 16), ("SS", c, c + 16), AL.add)
-            tt(("NEW", b, 64, 4), ("HB", c, c + 16), ("HC", c, c + 16), AL.add)
-        qz(hw, CO + G, 128, "NEW")
-        pick(hn, CO, hw, 32, 96, "OS%d" % t, 0, 1)
+            c, h = 16 * b, ("PS", 512 * b, 512 * b + 16)
+            if b < 3:
+                act(("SS", c, c + 16), ("PS", 512 * b + 16, 512 * b + 32), AF.Copy)
+                tt(("HB", c, c + 16), h, ("SS", c, c + 16), AL.add)
+                h = ("HB", c, c + 16)
+            tt(("NEW", b, 64, 4), h, ("HC", c, c + 16), AL.add)
+        qz(hn, CO, 128, "NEW")
         if t + 1 < R:
             for k in "cs":
-                spread(t + 1, k, [efar, enear])
-            pick("CA%d" % (t + 1), G * rank, hw, 32, 96, "OS%d" % t, 0, 1)
+                spread(t + 1, k, [efar, enear], h0)
+            lcopy("y", "CA%d" % (t + 1), G * rank, hn, CO, G)
+            for b in range(4):
+                act(("WN", 64 + 16 * b, 80 + 16 * b), ("NEW", b, 64, 4), AF.Copy)
         else:
             i = (hn + "c", CO, CO + G)
             dma("y", T.oc[:, 0:4 * G], view(i).bitcast(dt.uint8), [i], [])
@@ -485,17 +504,12 @@ def rank_program(g, core, T, topo):
         if t == 0:
             qz("WQ", 0, 128, "WT")
         if t + 1 < R:
-            qz("PK%d" % (t + 1), 0, 128, "ZT")
-            qz("HW%d" % (t + 2), 0, 176, "ZT")
+            qz("PK%d" % (t + 1), 0, 144, "ZT")
+            qz("HW%d" % (t + 2), 0, 128, "ZT")
         mm(6, "WQ", 0, pk, 0)
-        act(("YO", 32 * t, 32 * t + 32, 2), ("PS", 3072, 3072 + 16), AF.Copy)
-        act(("YO", 32 * t + 1, 32 * t + 32, 2), ("PS", 3072 + 32, 3072 + 48), AF.Copy)
+        cp(("YO", 32 * t, 32 * t + 32, 2), ("PS", 3072, 3072 + 16))
+        cp(("YO", 32 * t + 1, 32 * t + 32, 2), ("PS", 3072 + 32, 3072 + 48))
         dma("y", T.y[:, 32 * t:32 * t + 32], T.YO[:, 32 * t:32 * t + 32], [("YO", 32 * t, 32 * t + 32)], [])
-        for i in range(2):
-            ts(("XB", 0, 10), (kb, 0, 10), ("MM", 2 * i, 2 * i + 1), AL.is_equal)
-            tt(("XB", 0, 10), ("XB", 0, 10), (kn, 0, 10), AL.mult)
-            red(("SN", i, i + 1), ("XB", 0, 10), AL.add)
-        ts(("ID%d" % t, 0, 2), ("SN", 0, 2), -1.0, AL.add)
         dma("y", T.ids[:, 32 * t:32 * t + 32], T["ID%d" % t][0:16, 0:2], [("ID%d" % t, 0, 2)], [])
 
     for q in cnt:

@@ -5,7 +5,7 @@ G, TOK, CAPP, R, H = 16, 96, 48, 3, 4
 TW = 544
 BIGW = 16384
 CO = 48
-BY0, BYH = {"c": 0, "s": 2}, {"c": 2, "s": 1}
+BY0, BYH = {"c": 0, "s": 1}, {"c": 3, "s": 2}
 
 F32, BF, I32, U16, COD, PLN = "float32", "bfloat16", "int32", "uint16", "float8_e4m3fn_x4", "uint8"
 SCRATCH = {"PS": ("psum", [128, 4096], F32)}
@@ -22,14 +22,17 @@ def _mx(name, n):
 
 
 for _n, _w in (("CBT", 512), ("X0", 512), ("X12", 768), ("WT", 512), ("ZT", 704), ("TRT", 512), ("E25", 2048), ("THR", 128), ("KP", 128),
-               ("KO", 128), ("HI", 32), ("LO", 32), ("OT", 512), ("NT", 512), ("NO", 512), ("YF", 32), ("Y", 544), ("NEW", 512), ("J", 512), ("JA", 256)):
+               ("KO", 128), ("HI", 40), ("LO", 40), ("OT", 512), ("NT", 512), ("NO", 512), ("YF", 40), ("Y", 552), ("NEW", 512), ("J", 512)):
     _buf(_n, _w, BF)
-for _n, _w in (("RM", 128), ("NEG", 128), ("DV", 128), ("TA", 256), ("QC", 1), ("KC", 2), ("RB", 512), ("WV", 4), ("SC", 128), ("CC", 8), ("XA", 8),
-               ("OW", 2), ("LK", 2), ("MM", 4), ("TT", 4), ("SS", 64), ("HB", 64), ("WN", 128), ("HC", 64), ("BQ", 4), ("YO", 96)):
+for _n, _w in (("RM", 128), ("NEG", 128), ("DV", 128), ("TA", 256), ("QC", 1), ("KZ", 4), ("RB", 512), ("WV", 4), ("SC", 128), ("CC", 8), ("XA", 12),
+               ("OW", 12), ("AA", 4), ("BB", 4), ("CO", 2), ("FL", 12), ("TB", 4), ("TU", 2), ("HF", 2), ("TT", 4), ("IV", 8),
+               ("SS", 64), ("HB", 64), ("WN", 128), ("HC", 64), ("BQ", 4), ("YO", 96)):
     _buf(_n, _w, F32)
-for _n, _w in (("QI", 1), ("QJ", 1), ("NV", 96), ("RI", 128), ("WI", 4), ("WJ", 4)):
+for _n, _w in (("QI", 1), ("QJ", 1), ("NJ", 6), ("NV", 120), ("RI", 128)):
     _buf(_n, _w, I32)
-for _n, _w in (("XQ0", 128), ("XQ12", 192), ("WQ", 128), ("TRQ", 128), ("E25Q", 512), ("OC", 128), ("NQ", 128), ("NOQ", 128), ("YQ", 136),
+for _n, _w in (("LI", 6), ("LC", 2)):
+    _buf(_n, _w, U16)
+for _n, _w in (("XQ0", 128), ("XQ12", 192), ("WQ", 128), ("TRQ", 128), ("E25Q", 512), ("OC", 128), ("NQ", 128), ("NOQ", 128), ("YQ", 138),
                ("HX0", 96), ("HX12", 192)):
     _mx(_n, _w)
 for _t in range(R):
@@ -37,9 +40,8 @@ for _t in range(R):
     _mx("CA%d" % _t, 128)
     _mx("PP%d" % _t, 32)
     _mx("PK%d" % _t, 144)
-    _buf("NP%d" % _t, 2, F32)
+    _buf("NP%d" % _t, 12, F32)
     _buf("LN%d" % _t, 2, F32)
-    _buf("KB%d" % _t, 8, F32)
     _buf("ID%d" % _t, 2, F32)
     _buf("OP%d" % _t, 2, U16)
     _buf("OF%d" % _t, 4, U16)
@@ -54,7 +56,7 @@ def _bits(es):
     return sum(1 << e for e in es)
 
 
-def _helper_of(core, T, topo, i=0):
+def _helper_of(core, T, topo, i):
     return [c for c in topo.cores_of(core) if T.rank_of(c) is None and topo.die(c) == topo.die(core)][i]
 
 
@@ -76,7 +78,7 @@ def _dst(c, topo):
 
 
 def _relay(t):
-    return ("HX0", 0) if t == 0 else ("HX12", TOK * (t - 1))
+    return ("Q0", 0) if t == 0 else ("Q12", TOK * (t - 1))
 
 
 def _far(rank, T, topo):
@@ -89,37 +91,33 @@ def _near_engines(a, b, far, topo):
     return [e for e in topo.engines(a, b) if e not in topo.engines(a, far)]
 
 
-def _helper(g, core, rank, T, topo):
+def _hand_on(g, core, rank, T, topo, k):
     me = T.cores[rank]
     far = [r for r in _half(rank) if topo.chip(T.cores[r]) != topo.chip(me)]
     es = topo.engines(core, T.cores[far[0]])
     near = _near_engines(me, core, T.cores[far[0]], topo)
+    byt = (lambda v: v.bitcast(dt.uint8)) if k == "c" else (lambda v: v)
     n = 0
     for t in range(R):
-        for k in "cs":
-            g.wait_ge(T.sem["h%s%d" % (k, t)], len(near) if t == 0 else len(near) // 2)
-            dsts = []
-            for r in far:
-                o = _base(r) + TOK * (rank % H)
-                v = T["TK%d%s" % (t, k)][:, o:o + TOK]
-                dsts.append(v.bitcast(dt.uint8) if k == "c" else v)
-            nm, a = _relay(t)
-            v = T[nm + k][:, a:a + TOK]
-            src = v.bitcast(dt.uint8) if k == "c" else v
-            g.remote_dma_fused([RemoteDMATransfer(dst_ids=[_dst(T.cores[r], topo) for r in far], dma_engine_mask=_bits(es),
-                                                  remote_sem=T.sem["aT%d" % t], srcs=[src], dsts=dsts)], local_sem=T.sem.sent)
-            n += len(es)
+        g.wait_ge(T.sem["h%s%d" % (k, t)], len(near) if t == 0 else len(near) // 2)
+        dsts = []
+        for r in far:
+            o = _base(r) + TOK * (rank % H)
+            dsts.append(byt(T["TK%d%s" % (t, k)][:, o:o + TOK]))
+        nm, a = _relay(t)
+        g.remote_dma_fused([RemoteDMATransfer(dst_ids=[_dst(T.cores[r], topo) for r in far], dma_engine_mask=_bits(es),
+                                              remote_sem=T.sem["aT%d" % t], srcs=[byt(T["HX" + nm[1:] + k][:, a:a + TOK])], dsts=dsts)],
+                           local_sem=T.sem.sent)
+        n += len(es)
     mate = [r for r in range(len(T.cores)) if r != rank and topo.chip(T.cores[r]) == topo.chip(me)]
     en = _near_engines(core, T.cores[mate[0]], T.cores[far[0]], topo)
     for t in range(1, R):
-        for k in "cs":
-            last = _far(rank, T, topo)[-BYH[k]:]
-            g.wait_ge(T.sem["g%s%d" % (k, t)], len(near))
-            v = T["CA%d%s" % (t, k)][:, G * rank:G * rank + G]
-            v = v.bitcast(dt.uint8) if k == "c" else v
-            g.remote_dma_fused([RemoteDMATransfer(dst_ids=[_dst(T.cores[r], topo) for r in rs], dma_engine_mask=_bits(e), remote_sem=T.sem["aC%d" % t],
-                                                  srcs=[v], dsts=[v] * len(rs)) for e, rs in ((es, last), (en, mate))], local_sem=T.sem.sent)
-            n += len(es) + len(en)
+        last = _far(rank, T, topo)[-BYH[k]:]
+        g.wait_ge(T.sem["g%s%d" % (k, t)], len(near))
+        v = byt(T["CA%d%s" % (t, k)][:, G * rank:G * rank + G])
+        g.remote_dma_fused([RemoteDMATransfer(dst_ids=[_dst(T.cores[r], topo) for r in rs], dma_engine_mask=_bits(e), remote_sem=T.sem["aC%d" % t],
+                                              srcs=[v], dsts=[v] * len(rs)) for e, rs in ((es, last), (en, mate))], local_sem=T.sem.sent)
+        n += len(es) + len(en)
     g.wait_ge(T.sem.sent, n)
 
 
@@ -137,18 +135,18 @@ def rank_program(g, core, T, topo):
     rank = T.rank_of(core)
     if rank is None:
         for r in range(len(T.cores)):
-            if _helper_of(T.cores[r], T, topo) == core:
-                _helper(g, core, r, T, topo)
-            if _helper_of(T.cores[r], T, topo, 1) == core:
+            for i, k in enumerate("cs"):
+                if _helper_of(T.cores[r], T, topo, i) == core:
+                    _hand_on(g, core, r, T, topo, k)
+            if _helper_of(T.cores[r], T, topo, 2) == core:
                 _first(g, core, r, T, topo)
         return
     AL, AF, AX = AluOpType, ActivationFunctionType, AxisListType.X
     half, sl = rank // H, rank % H
     part = (rank + H) % (2 * H)
-    own = (rank, part)
+    both = (rank, part)
     tb, lb = _base(rank), _land(rank)
-    zo = tb + 4 * TOK + (64 if half == 0 else 0)
-    up = 64 if half == 0 else 0
+    z = tb + 4 * TOK
     on1, ln1 = (H * TOK + 1, 2 * H * TOK + 1) if half == 0 else (2 * H * TOK + 1, H * TOK + 1)
     eng = {"v": g.vector, "s": g.scalar, "p": g.tensor, "g": g, "y": g.sync}
     done = {"v": "vd", "s": "sd", "p": "pd", "g": "gd"}
@@ -231,6 +229,11 @@ def rank_program(g, core, T, topo):
     def scan(out, d0, d1, ini, o0, o1):
         return op("v", lambda v: v.tensor_tensor_scan(view(out), view(d0), view(d1), ini, o0, o1), [d0, d1], [out])
 
+    def top2(nm, x):
+        scan((nm, 2, 11), x, ("NEG", 0, 9), 0.0, AL.max, AL.max)
+        tt(("XA", 1, 9), (x[0], x[1] + 1, x[2]), (nm, 2, 10), AL.min)
+        red((nm, 11, 12), ("XA", 1, 9), AL.max)
+
     def qz(nm, a, n, tile, ta=0):
         oc, os, i = (nm + "c", a, a + n), (nm + "s", a, a + n), (tile, ta, ta + 4 * n)
         return op("v", lambda v: v.quantize_mx(view(oc), view(os), view(i)), [i], [oc, os])
@@ -255,14 +258,6 @@ def rank_program(g, core, T, topo):
         eng[q].dma_start(out, in_).then_inc(T.sem[tok[0]], 16)
         after(q, tok, rd, wr)
 
-    def lcopy(q, dst, da, src, sa, n):
-        for k in "cs":
-            i, o = (src + k, sa, sa + n), (dst + k, da, da + n)
-            vi, vo = view(i), view(o)
-            if k == "c":
-                vi, vo = vi.bitcast(dt.uint8), vo.bitcast(dt.uint8)
-            dma(q, vo, vi, [i], [o])
-
     def iota(x, pat, base, ch):
         if SCRATCH[x[0]][2] == I32:
             op("g", lambda e: e.iota(view(x), pat, base, ch), [], [x])
@@ -280,7 +275,7 @@ def rank_program(g, core, T, topo):
     efar = topo.engines(core, T.cores[far[0]])
     enear = _near_engines(core, T.cores[near[0]], T.cores[far[0]], topo)
     hn2 = len(enear) // 2
-    h0, h1 = _helper_of(core, T, topo), _helper_of(core, T, topo, 1)
+    hand = {"c": _helper_of(core, T, topo, 0), "s": _helper_of(core, T, topo, 1)}
     sent = [0]
 
     def send(transfers):
@@ -307,13 +302,12 @@ def rank_program(g, core, T, topo):
         send(tr)
 
     def tokens(t, k, es):
-        nm, a = ("XQ0", 0) if t == 0 else ("XQ12", TOK * (t - 1))
-        hx, ha = _relay(t)
-        src = (nm + k, a, a + TOK)
+        nm, a = _relay(t)
+        src = ("X" + nm + k, a, a + TOK)
         o = tb + TOK * sl
         tr = []
         if es[0]:
-            tr.append((es[0], "h%s%d" % (k, t), src, [(h0, (hx + k, ha, ha + TOK))]))
+            tr.append((es[0], "h%s%d" % (k, t), src, [(hand[k], ("HX" + nm[1:] + k, a, a + TOK))]))
         if es[1]:
             tr.append((es[1], "aT%d" % t, src, [(T.cores[r], ("TK%d%s" % (t, k), o, o + TOK)) for r in near]))
         send(tr)
@@ -324,42 +318,41 @@ def rank_program(g, core, T, topo):
     dma("s", T.WT[:], T.w[:], [], [("WT", 0, 512)])
     iota(("DV", 0, 128), [[1, 128]], 0, -1)
     for e in range(2):
-        iota(("THR", 64 * e, 64 * e + 64), [[1, G], [1, 4]], G * own[e], 0)
+        iota(("THR", 64 * e, 64 * e + 64), [[1, G], [1, 4]], G * both[e], 0)
     iota(("KP", 0, 128), [[0, 8], [1, 16]], G * part, 0)
     iota(("KO", 0, 128), [[0, 8], [1, 16]], G * rank, 0)
     iota(("RI", 0, 128), [[0, 4], [1, 32]], 0, 0)
     iota(("QI", 0, 1), [[0, 1]], 0, 1)
-    iota(("NV", 0, 32), [[0, 8], [-TOK, 4]], 4 * TOK, -1)
+    iota(("NJ", 0, 6), [[16, 6]], 0, 0)
+    iota(("NV", 0, 40), [[0, 10], [TOK, 4]], TOK, -1)
     fill(("CBT", 4 * G, 512), 0.0)
     fill(("ZT", 0, 704), 0.0)
     for t in range(R):
         qz("TK%d" % t, tb + 4 * TOK, 128, "ZT")
     qz("HW0", 0, 128, "ZT")
     fill(("X0", 4 * TOK, 512), 0.0)
-    qz("HW0", CO, 128, "CBT")
     qz("XQ0", 0, 128, "X0")
+    qz("HW0", CO, 128, "CBT")
+    for k in "cs":
+        tokens(0, k, [enear, []])
     spread(0, "c", [efar, []], None)
-    tokens(0, "c", [enear, []])
-    spread(0, "s", [efar, enear], h1)
-    tokens(0, "s", [enear, []])
+    spread(0, "s", [efar, enear], _helper_of(core, T, topo, 2))
     for k in "cs":
         spread(0, k, [[], enear], "mate")
     for k in "cs":
         tokens(0, k, [[], enear])
-    lcopy("y", "CA0", G * rank, "HW0", CO, G)
-    lcopy("s", "TK0", tb + TOK * sl, "XQ0", 0, TOK)
     qz("XQ12", 0, 2 * TOK, "X12")
     for t in range(1, R):
         for k in "cs":
             tokens(t, k, [enear[hn2:], enear[:hn2]])
-        lcopy("y", "TK%d" % t, tb + TOK * sl, "XQ12", TOK * (t - 1), TOK)
+    camec = 2 * (len(efar) * len(far) + len(enear) * len(near))
     for t in range(R):
         came = 2 * (len(enear) if t == 0 else hn2) + 2 * len(efar) * len([r for r in _half(rank) if r in far])
         for s in range(H):
             if s != sl:
                 ext("aT%d" % t, came, [("TK%d%s" % (t, k), tb + TOK * s, tb + TOK * s + TOK) for k in "cs"])
         for r in peers:
-            ext("aC%d" % t, 2 * (len(efar) * len(far) + len(enear) * len(near)), [("CA%d%s" % (t, k), G * r, G * r + G) for k in "cs"])
+            ext("aC%d" % t, camec, [("CA%d%s" % (t, k), G * r, G * r + G) for k in "cs"])
         ext("aK%d" % t, 2 * len(efar), [("TK%d%s" % (t, k), lb, lb + 32) for k in "cs"])
         ext("aL%d" % t, len(efar), [("LN%d" % t, 0, 2)])
 
@@ -367,10 +360,10 @@ def rank_program(g, core, T, topo):
     for b in range(4):
         act(("E25", 512 * b, 512 * b + 512), ("ZT", 0, 512), AF.Copy)
     act(("NEG", 0, 128), ("ZT", 0, 128), AF.Identity, bias=-1e29)
-    act(("YF", 0, 32), ("ZT", 0, 32), AF.Copy)
+    act(("YF", 0, 40), ("ZT", 0, 40), AF.Copy)
     for e in range(2):
         for i in range(2):
-            iota(("THR", 64 * e + 2 + i, 64 * e + 64, 4), [[0, G]], G * (own[e] + i), 0)
+            iota(("THR", 64 * e + 2 + i, 64 * e + 64, 4), [[0, G]], G * (both[e] + i), 0)
     ts(ta, dv, 1.0, AL.is_ge, 128.0, AL.mult)
     ts(tc, dv, 0.0, AL.is_equal, float(BIGW), AL.mult)
     ts(("TRT", 2, 512, 4), dv, 1.0, AL.is_ge)
@@ -382,17 +375,23 @@ def rank_program(g, core, T, topo):
         ts(("E25", 512 * b + b, 512 * b + 512, 4), dv, 0.0, AL.is_equal, 0.25, AL.mult)
     ts(("QJ", 0, 1), ("QI", 0, 1), 15, AL.bitwise_and)
     cp(("QC", 0, 1), ("QJ", 0, 1))
+    ts(("LI", 0, 6), ("NJ", 0, 6), ("QC", 0, 1), AL.add)
+    ts(("LC", 0, 1), ("QC", 0, 1), float(CO), AL.add)
+    pick("CA0", G * rank, "HW0", 0, 64 + G, "LC", 0, 1)
+    for t in range(R):
+        nm, a = _relay(t)
+        pick("TK%d" % t, tb + TOK * sl, "X" + nm, a, a + TOK, "LI", 0, 6)
     ts(("RM", 0, 128), ("RI", 0, 128), 0.5, AL.is_ge)
     fill(("TRT", 4 * TOK, 512), 0.0)
     op("v", lambda v: v.memset(T.TRT[TOK:128, :], 0.0), [], [("TRT", 0, 512)])
     qz("TRQ", 0, 128, "TRT")
-    ts(("NV", 32, 64), ("NV", 0, 32), 16.0, AL.add)
-    ts(("NV", 64, 96), ("NV", 32, 64), 5, AL.arith_shift_right)
-    ts(("HI", 0, 32), ("NV", 64, 96), 32.0, AL.mult)
-    tt(("LO", 0, 32), ("NV", 0, 32), ("HI", 0, 32), AL.subtract)
-    for i in range(2):
-        act(("KC", i, i + 1), ("QC", 0, 1), AF.Identity, bias=float((32 - 16 * i + (4 * TOK if half else 0)) * 1024 + ln1), scale=-1024.0)
-    act(("Y", 64, 544), ("ZT", 0, 480), AF.Copy)
+    ts(("NV", 40, 80), ("NV", 0, 40), 16.0, AL.add)
+    ts(("NV", 80, 120), ("NV", 40, 80), 5, AL.arith_shift_right)
+    ts(("HI", 0, 40), ("NV", 80, 120), 32.0, AL.mult)
+    tt(("LO", 0, 40), ("NV", 0, 40), ("HI", 0, 40), AL.subtract)
+    for i, c in enumerate((lb - z, lb + 16 - z, lb)):
+        act(("KZ", i, i + 1), ("QC", 0, 1), AF.Identity, bias=float(c))
+    act(("Y", 80, 552), ("ZT", 0, 472), AF.Copy)
     for b in range(4):
         act(("BQ", b, b + 1), ("QC", 0, 1), AF.Identity, bias=float(16 * b))
         act(("WN", 64 + 16 * b, 80 + 16 * b), ("CBT", b, 64, 4), AF.Copy)
@@ -400,103 +399,148 @@ def rank_program(g, core, T, topo):
     qz("PK0", 0, 144, "ZT")
     qz("E25Q", 0, 512, "E25")
 
+    def score(s):
+        r = ("RB", 128 * s, 128 * s + 128)
+        scan(r, ("PS", 512 * s, 512 * s + 128), ("NEG", 0, 128), -1e29, AL.max, AL.max)
+        act(("J", 128 * s, 128 * s + 128), r, AF.Sign, bias=("RB", 128 * s + 127, 128 * s + 128), scale=-1.0, acc=("WV", s, s + 1))
+
+    def thr(s):
+        ts(("OT", 128 * s, 128 * s + 128), ("THR", 0, 128), ("WV", s, s + 1), AL.is_le)
+
+    def hot(s):
+        ts(("NT", s, 512, 4), ("KP", 0, 128), ("WV", s, s + 1), AL.is_equal)
+
+    def mine(s):
+        ts(("NO", s, 512, 4), ("KO", 0, 128), ("WV", s, s + 1), AL.is_equal)
+
     for t in range(R):
         tk, ca, pp, pk, hw, hn = "TK%d" % t, "CA%d" % t, "PP%d" % t, "PK%d" % t, "HW%d" % t, "HW%d" % (t + 1)
-        np_, ln, kb = "NP%d" % t, "LN%d" % t, "KB%d" % t
+        np_, ln = "NP%d" % t, "LN%d" % t
         for s in range(H):
-            mm(s, tk, tb + TOK * s, ca, 0)
+            mm(s, tk, tb + TOK * (H - 1 - s), ca, 0)
         for s in range(H):
-            r = ("RB", 128 * s, 128 * s + 128)
-            scan(r, ("PS", 512 * s, 512 * s + 128), ("NEG", 0, 128), -1e29, AL.max, AL.max)
-            act(("J", 128 * s, 128 * s + 128), r, AF.Sign, bias=("RB", 128 * s + 127, 128 * s + 128), scale=-1.0, acc=("WV", s, s + 1))
-        for s in range(H):
-            ts(("OT", 128 * s, 128 * s + 128), ("THR", 0, 128), ("WV", s, s + 1), AL.is_le)
+            score(s)
+        for f, s in ((thr, 0), (thr, 1), (hot, 0), (thr, 2), (hot, 1), (thr, 3)):
+            f(s)
         qz("OC", 0, 128, "OT")
         mm(4, "TRQ", 0, "OC", 0)
-        for s in range(H):
-            o, w, j = ("NT", s, 512, 4), ("WV", s, s + 1), ("JA", 128 * (s % 2), 128 * (s % 2) + 128)
-            if s < 3:
-                ts(o, ("KP", 0, 128), w, AL.is_equal)
-            else:
-                act(j, ("KP", 0, 128), AF.Abs, bias=w, scale=-1.0)
-                act(o, j, AF.Relu, bias=1.0, scale=-1.0)
+        hot(2)
+        hot(3)
         if t == 0:
             act(("NEW", 64, 512), ("ZT", 0, 448), AF.Copy)
-        qz("NQ", 0, 128, "NT")
         scan(("SC", 0, 128), ("RM", 0, 128), ("PS", 2048, 2176), 0.0, AL.mult, AL.max)
+        qz("NQ", 0, 128, "NT")
         mk = ("SC", 31, 128, 32)
         for i in range(2):
-            lo, cc = BIGW + 128 * i, ("CC", 4 * i, 4 * i + 4)
-            ts(cc, mk, float(lo + CAPP - 1), AL.min, float(lo), AL.max)
-            tt(("YF", 16 * i, 16 * i + 16, 5), cc, mk, AL.is_equal)
-        tt(("Y", 0, 32), ("YF", 0, 32), ("HI", 0, 32), AL.mult)
-        tt(("Y", 32, 64), ("YF", 0, 32), ("LO", 0, 32), AL.mult)
-        qz("YQ", 0, 136, "Y")
+            ts(("CC", 4 * i, 4 * i + 4), mk, float(BIGW + 128 * i + CAPP - 1), AL.min, float(BIGW + 128 * i), AL.max)
+        for i in range(2):
+            tt(("YF", 20 * i, 20 * i + 20, 5), ("CC", 4 * i, 4 * i + 4), mk, AL.is_equal)
+        mine(0)
+        tt(("Y", 0, 40), ("YF", 0, 40), ("HI", 0, 40), AL.mult)
+        tt(("Y", 40, 80), ("YF", 0, 40), ("LO", 0, 40), AL.mult)
+        mine(1)
+        qz("YQ", 0, 138, "Y")
         mm(5, "NQ", 0, "YQ", 0, True, False)
-        mm(5, "NQ", 0, "YQ", 8, False, True)
-        lp = ("PS", 2560, 2568)
-        red((np_, 0, 1), lp, AL.max)
-        ts(("XA", 0, 8), lp, (np_, 0, 1), AL.is_lt)
-        tt(("XA", 0, 8), ("XA", 0, 8), lp, AL.mult)
-        red((np_, 1, 2), ("XA", 0, 8), AL.max)
-        ts(("OP%d" % t, 0, 2), (np_, 0, 2), -1.0, AL.mult, float(4 * TOK), AL.add)
-        send([(efar, "aL%d" % t, (np_, 0, 2), [(T.cores[part], (ln, 0, 2))])])
+        mm(5, "NQ", 0, "YQ", 10, False, True)
+        mine(2)
+        mine(3)
+        qz("NOQ", 0, 128, "NO")
+        mm(6, "NOQ", 0, "YQ", 0, True, False)
+        mm(6, "NOQ", 0, "YQ", 10, False, True)
+        top2(np_, ("PS", 2560, 2569))
+        ts(("OP%d" % t, 0, 2), (np_, 10, 12), -1.0, AL.mult, float(4 * TOK), AL.add)
+        send([(efar, "aL%d" % t, (np_, 10, 12), [(T.cores[part], (ln, 0, 2))])])
         pick(pp, 0, tk, tb, (lb if half == 0 else TW), "OP%d" % t, 0, 2)
         for k in "cs":
             send([(efar, "aK%d" % t, (pp + k, 0, 32), [(T.cores[part], (tk + k, _land(part), _land(part) + 32))])])
-        for s in range(H):
-            ts(("NO", s, 512, 4), ("KO", 0, 128), ("WV", s, s + 1), AL.is_equal)
-        qz("NOQ", 0, 128, "NO")
-        mm(6, "NOQ", 0, "YQ", 0, True, False)
-        mm(6, "NOQ", 0, "YQ", 8, False, True)
-        lo = ("PS", 3072, 3080)
-        ts(("XA", 0, 8), lo, 0.5, AL.is_ge, float(1024 * up + on1), AL.mult)
-        ts((kb, 0, 8), lo, 1023.0, AL.mult)
-        tt((kb, 0, 8), (kb, 0, 8), ("XA", 0, 8), AL.add)
-        o1, o2, l1, l2 = ("OW", 0, 1), ("OW", 1, 2), ("LK", 0, 1), ("LK", 1, 2)
-        red(o1, (kb, 0, 8), AL.max)
-        ts(("XA", 0, 8), (kb, 0, 8), o1, AL.is_lt)
-        tt(("XA", 0, 8), ("XA", 0, 8), (kb, 0, 8), AL.mult)
-        red(o2, ("XA", 0, 8), AL.max)
+        top2("OW", ("PS", 3072, 3081))
+        n1, n2, n12 = ("OW", 10, 11), ("OW", 11, 12), ("OW", 10, 12)
+        k1z, k2z, k1 = ("KZ", 0, 1), ("KZ", 1, 2), ("KZ", 2, 3)
+        b0, b1, b2, c1, c2 = ("BB", 0, 1), ("BB", 1, 2), ("BB", 2, 3), ("CO", 0, 1), ("CO", 1, 2)
+        fl = [("FL", i, i + 1) for i in range(12)]
+        ts(("AA", 0, 3, 2), n12, -1.0, AL.mult, float(z), AL.add)
+        ts(fl[0], n2, 0.5, AL.is_lt, n1, AL.mult)
+        if half == 0:
+            ts(b0, n1, 0.5, AL.is_lt, k1z, AL.mult)
+            ts(fl[1], n2, 0.5, AL.is_lt, k1z, AL.mult)
+            ts(("AA", 1, 2), fl[0], -1.0, AL.mult, ("AA", 2, 3), AL.add)
+            ts(c1, n1, 0.5, AL.is_lt, 16.0, AL.mult)
+            ts(b1, fl[1], fl[0], AL.add)
+            ts(b2, fl[1], b0, AL.subtract)
+            ts(c2, n1, 0.5, AL.is_lt, k2z, AL.mult)
+        else:
+            ts(b0, n1, k1z, AL.add)
+            ts(b2, n2, n1, AL.subtract)
+            ts(("AA", 1, 2), fl[0], -1.0, AL.mult, ("AA", 2, 3), AL.add)
+            ts(fl[1], n1, 0.5, AL.is_ge, b0, AL.mult)
+            ts(c2, b0, 16.0, AL.add)
+            ts(fl[2], fl[1], -1.0, AL.mult, k1, AL.add)
+            ts(c1, fl[1], 16.0, AL.add)
+            ts(b1, fl[2], ("AA", 1, 2), AL.subtract)
+        ts(fl[3], n1, 0.5, AL.is_lt, 64.0, AL.mult)
+        v1, v2, v12 = ("IV", 0, 1), ("IV", 1, 2), ("IV", 0, 2)
+        ts(("IV", 2, 4), n12, 0.5, AL.is_ge, float(on1), AL.mult)
+        if half == 0:
+            ts(fl[4], n1, 0.5, AL.is_lt)
+            ts(fl[5], n2, 0.5, AL.is_lt, fl[4], AL.subtract)
+        tt(v12, ("IV", 2, 4), n12, AL.subtract)
+        if half == 1:
+            ts(fl[4], v1, v2, AL.subtract)
         for b in range(4):
             mm(7, "E25Q", 128 * b, hw, CO - 16 * b, b == 0, b == 3)
         act(("WN", 0, 64), ("PS", 3584, 3584 + 64), AF.Copy, scale=2.0)
+        h1, h2, of = ("HF", 0, 1), ("HF", 1, 2), "OF%d" % t
+        ts(("HF", 0, 2), (ln, 0, 2), 0.5, AL.is_ge)
+        ts(("TB", 0, 3), ("BB", 0, 3), h1, AL.mult)
+        ts(("TU", 0, 2), ("CO", 0, 2), h2, AL.mult)
+        ts((of, 0, 1), ("AA", 0, 1), ("TB", 0, 1), AL.add)
         for i in range(2):
-            ts(("LK", i, i + 1), (ln, i, i + 1), 0.5, AL.is_ge, ("KC", i, i + 1), AL.mult)
-        tt(("LK", 0, 2), ("LK", 0, 2), (ln, 0, 2), AL.subtract)
-        ts(("TT", 2, 3), l1, o1, AL.min, o2, AL.max)
-        ts(("MM", 0, 1), l1, o1, AL.max)
-        ts(("MM", 2, 3), l2, ("TT", 2, 3), AL.max)
-        ts(("TT", 0, 1), ("MM", 2, 3), 0.5, AL.is_lt, ("MM", 0, 1), AL.mult)
-        tt(("MM", 1, 2), ("TT", 0, 1), ("MM", 2, 3), AL.add)
-        ts(("OF%d" % t, 0, 3), ("MM", 0, 3), -1.0 / 1024, AL.mult, zo + 0.375, AL.add)
+            ts((of, 1 + i, 2 + i), ("AA", 1 + i, 2 + i), ("TB", 1 + i, 2 + i), AL.add, ("TU", i, i + 1), AL.add)
+
+        def number():
+            idn = "ID%d" % t
+            ts(("IV", 4, 6), (ln, 0, 2), -1.0, AL.mult, float(ln1), AL.add)
+            if half == 0:
+                tt(("IV", 6, 8), ("IV", 4, 6), ("HF", 0, 2), AL.mult)
+                ts(fl[6], ("IV", 6, 7), fl[5], AL.mult, v2, AL.add)
+                ts(fl[8], ("IV", 6, 7), fl[4], AL.mult, v1, AL.add)
+                ts(fl[9], ("IV", 7, 8), fl[4], AL.mult, fl[6], AL.add)
+            else:
+                ts(fl[6], h1, 0.5, AL.is_lt, v1, AL.mult)
+                tt(("IV", 6, 8), ("IV", 4, 6), ("HF", 0, 2), AL.mult)
+                ts(fl[7], h1, fl[4], AL.mult, v2, AL.add)
+                ts(fl[8], fl[6], ("IV", 6, 7), AL.add)
+                ts(fl[10], h2, 0.5, AL.is_lt, fl[7], AL.mult)
+                ts(fl[9], fl[10], ("IV", 7, 8), AL.add)
+            ts((idn, 0, 2), ("FL", 8, 10), -1.0, AL.add)
+
+        if t + 1 == R:
+            number()
         pick(pk, 0, tk, 0, TW, "OF%d" % t, 0, 3)
         for b in range(3):
             mm(b, "E25Q", 128 * b, pk, 0)
         mm(3, "E25Q", 384, pk, 16, True, False)
         mm(3, "E25Q", 384, pk, 0, False, True)
-        ts(("TT", 1, 2), ("MM", 0, 1), 0.5, AL.is_lt, 64.0, AL.mult)
+        ts(("TT", 1, 2), h1, 0.5, AL.is_lt, fl[3], AL.mult)
         ts(("OS%d" % t, 0, 4), ("BQ", 0, 4), ("TT", 1, 2), AL.add)
         w, o, h = ("WN", 0, 128), ("OS%d" % t, 0, 4), ("HC", 0, 64)
         op("s", lambda q, w=w, o=o, h=h: q.activation(view(h), view(w).indirect(view(o)), AF.Copy), [w, o], [h])
-        cp(("WI", 0, 3), ("MM", 0, 3))
-        ts(("WJ", 0, 3), ("WI", 0, 3), 1023, AL.bitwise_and)
-        ts(("ID%d" % t, 0, 2), ("WJ", 0, 3, 2), -1.0, AL.add)
-        for b in range(4):
+        for f, b in (("h", 0), ("h", 1), ("n", 0), ("h", 2), ("n", 1), ("n", 3), ("n", 2)):
             c, h = 16 * b, ("PS", 512 * b, 512 * b + 16)
-            if b < 3:
+            if f == "h":
                 act(("SS", c, c + 16), ("PS", 512 * b + 16, 512 * b + 32), AF.Copy)
                 tt(("HB", c, c + 16), h, ("SS", c, c + 16), AL.add)
-                h = ("HB", c, c + 16)
-            tt(("NEW", b, 64, 4), h, ("HC", c, c + 16), AL.add)
+            else:
+                tt(("NEW", b, 64, 4), h if b == 3 else ("HB", c, c + 16), ("HC", c, c + 16), AL.add)
         qz(hn, CO, 128, "NEW")
         if t + 1 < R:
             for k in "cs":
-                spread(t + 1, k, [efar, enear], h0)
-            lcopy("y", "CA%d" % (t + 1), G * rank, hn, CO, G)
+                spread(t + 1, k, [efar, enear], hand[k])
+            pick("CA%d" % (t + 1), G * rank, hn, 0, 64 + G, "LC", 0, 1)
             for b in range(4):
                 act(("WN", 64 + 16 * b, 80 + 16 * b), ("NEW", b, 64, 4), AF.Copy)
         else:
+            dma("y", T.ids[:, 32 * t:32 * t + 32], T["ID%d" % t][0:16, 0:2], [("ID%d" % t, 0, 2)], [])
             i = (hn + "c", CO, CO + G)
             dma("y", T.oc[:, 0:4 * G], view(i).bitcast(dt.uint8), [i], [])
             for k in range(4):
@@ -509,8 +553,11 @@ def rank_program(g, core, T, topo):
         mm(6, "WQ", 0, pk, 0)
         cp(("YO", 32 * t, 32 * t + 32, 2), ("PS", 3072, 3072 + 16))
         cp(("YO", 32 * t + 1, 32 * t + 32, 2), ("PS", 3072 + 32, 3072 + 48))
+        if t + 1 < R:
+            number()
+            wait("y", ("aC%d" % (t + 1), camec))
+            dma("y", T.ids[:, 32 * t:32 * t + 32], T["ID%d" % t][0:16, 0:2], [("ID%d" % t, 0, 2)], [])
         dma("y", T.y[:, 32 * t:32 * t + 32], T.YO[:, 32 * t:32 * t + 32], [("YO", 32 * t, 32 * t + 32)], [])
-        dma("y", T.ids[:, 32 * t:32 * t + 32], T["ID%d" % t][0:16, 0:2], [("ID%d" % t, 0, 2)], [])
 
     for q in cnt:
         wait("g", (done[q], cnt[q]))

@@ -3,7 +3,8 @@ from concourse.mybir import dt, AluOpType, AxisListType, ActivationFunctionType
 
 G, TOK, CAPP, R, H = 16, 96, 48, 3, 4
 TW = 544
-BIGW = 16384
+MARK, OWN, STEP = 12288, 80, 64
+FIRST = MARK + OWN - (STEP // 2 - (CAPP - STEP // 2))
 CO = 48
 BY0, BYH = {"c": 0, "s": 1}, {"c": 3, "s": 2}
 
@@ -22,10 +23,11 @@ def _mx(name, n):
 
 
 for _n, _w in (("CBT", 512), ("X0", 512), ("X12", 768), ("WT", 512), ("ZT", 704), ("TRT", 512), ("E25", 2048), ("THR", 128), ("KP", 128),
-               ("KO", 128), ("HI", 40), ("LO", 40), ("OT", 512), ("NT", 512), ("NO", 512), ("YF", 40), ("Y", 552), ("NEW", 512), ("J", 512)):
+               ("KO", 128), ("HI", 40), ("LO", 40), ("OT", 512), ("NT", 512), ("NO", 512), ("YF", 40), ("Y", 552), ("NEW", 512), ("J", 512),
+               ("SC", 128)):
     _buf(_n, _w, BF)
-for _n, _w in (("RM", 128), ("NEG", 128), ("DV", 128), ("TA", 256), ("QC", 1), ("KZ", 4), ("RB", 512), ("WV", 4), ("SC", 128), ("CC", 8), ("XA", 12),
-               ("OW", 12), ("AA", 4), ("BB", 4), ("CO", 2), ("FL", 12), ("TB", 4), ("TU", 2), ("HF", 2), ("TT", 4), ("IV", 8),
+for _n, _w in (("RM", 128), ("NEG", 128), ("DV", 128), ("TA", 256), ("QC", 1), ("KZ", 4), ("RB", 512), ("WV", 4), ("OW", 18), ("AA", 4), ("BB", 4),
+               ("CO", 2), ("FL", 12), ("TB", 4), ("TU", 2), ("HF", 2), ("TT", 4), ("IV", 4), ("UU", 8), ("UV", 2),
                ("SS", 64), ("HB", 64), ("WN", 128), ("HC", 64), ("BQ", 4), ("YO", 96)):
     _buf(_n, _w, F32)
 for _n, _w in (("QI", 1), ("QJ", 1), ("NJ", 6), ("NV", 120), ("RI", 128)):
@@ -40,7 +42,7 @@ for _t in range(R):
     _mx("CA%d" % _t, 128)
     _mx("PP%d" % _t, 32)
     _mx("PK%d" % _t, 144)
-    _buf("NP%d" % _t, 12, F32)
+    _buf("NP%d" % _t, 18, F32)
     _buf("LN%d" % _t, 2, F32)
     _buf("ID%d" % _t, 2, F32)
     _buf("OP%d" % _t, 2, U16)
@@ -212,16 +214,13 @@ def rank_program(g, core, T, topo):
         return op("v", lambda v: v.tensor_copy(view(out), view(a)), [a], [out])
 
     def act(out, a, f, bias=0.0, scale=1.0, acc=None):
-        rd = [a] + ([bias] if isap(bias) else [])
-        b = view(bias) if isap(bias) else bias
+        rd = [a] + [x for x in (bias, scale) if isap(x)]
+        b, c = [view(x) if isap(x) else x for x in (bias, scale)]
         if acc is not None:
-            return op("s", lambda s: s.activation(view(out), view(a), f, bias=b, scale=scale, accum_out=view(acc)), rd, [out, acc])
+            return op("s", lambda s: s.activation(view(out), view(a), f, bias=b, scale=c, accum_out=view(acc)), rd, [out, acc])
         if f == AF.Copy:
-            return op("s", lambda s: s.activation(view(out), view(a), f, scale=scale), rd, [out])
-        return op("s", lambda s: s.activation(view(out), view(a), f, bias=b, scale=scale), rd, [out])
-
-    def red(out, a, o):
-        return op("v", lambda v: v.tensor_reduce(view(out), view(a), AX, o), [a], [out])
+            return op("s", lambda s: s.activation(view(out), view(a), f, scale=c), rd, [out])
+        return op("s", lambda s: s.activation(view(out), view(a), f, bias=b, scale=c), rd, [out])
 
     def fill(x, c):
         return op("v", lambda v: v.memset(view(x), c), [], [x])
@@ -230,9 +229,8 @@ def rank_program(g, core, T, topo):
         return op("v", lambda v: v.tensor_tensor_scan(view(out), view(d0), view(d1), ini, o0, o1), [d0, d1], [out])
 
     def top2(nm, x):
-        scan((nm, 2, 11), x, ("NEG", 0, 9), 0.0, AL.max, AL.max)
-        tt(("XA", 1, 9), (x[0], x[1] + 1, x[2]), (nm, 2, 10), AL.min)
-        red((nm, 11, 12), ("XA", 1, 9), AL.max)
+        scan((nm, 0, 17, 2), x, ("NEG", 0, 9), 0.0, AL.max, AL.max)
+        scan((nm, 3, 18, 2), (x[0], x[1] + 1, x[2]), (nm, 0, 15, 2), 0.0, AL.max, AL.min)
 
     def qz(nm, a, n, tile, ta=0):
         oc, os, i = (nm + "c", a, a + n), (nm + "s", a, a + n), (tile, ta, ta + 4 * n)
@@ -317,11 +315,6 @@ def rank_program(g, core, T, topo):
     dma("y", T.X12[:], T.x[:, 4 * TOK:12 * TOK], [], [("X12", 0, 8 * TOK)])
     dma("s", T.WT[:], T.w[:], [], [("WT", 0, 512)])
     iota(("DV", 0, 128), [[1, 128]], 0, -1)
-    for e in range(2):
-        iota(("THR", 64 * e, 64 * e + 64), [[1, G], [1, 4]], G * both[e], 0)
-    iota(("KP", 0, 128), [[0, 8], [1, 16]], G * part, 0)
-    iota(("KO", 0, 128), [[0, 8], [1, 16]], G * rank, 0)
-    iota(("RI", 0, 128), [[0, 4], [1, 32]], 0, 0)
     iota(("QI", 0, 1), [[0, 1]], 0, 1)
     iota(("NJ", 0, 6), [[16, 6]], 0, 0)
     iota(("NV", 0, 40), [[0, 10], [TOK, 4]], TOK, -1)
@@ -362,12 +355,17 @@ def rank_program(g, core, T, topo):
     act(("NEG", 0, 128), ("ZT", 0, 128), AF.Identity, bias=-1e29)
     act(("YF", 0, 40), ("ZT", 0, 40), AF.Copy)
     for e in range(2):
+        iota(("THR", 64 * e, 64 * e + 64), [[1, G], [1, 4]], G * both[e], 0)
+    iota(("KP", 0, 128), [[0, 8], [1, 16]], G * part, 0)
+    iota(("RI", 0, 128), [[0, 4], [1, 32]], 0, 0)
+    iota(("KO", 0, 128), [[0, 8], [1, 16]], G * rank, 0)
+    for e in range(2):
         for i in range(2):
             iota(("THR", 64 * e + 2 + i, 64 * e + 64, 4), [[0, G]], G * (both[e] + i), 0)
-    ts(ta, dv, 1.0, AL.is_ge, 128.0, AL.mult)
-    ts(tc, dv, 0.0, AL.is_equal, float(BIGW), AL.mult)
-    ts(("TRT", 2, 512, 4), dv, 1.0, AL.is_ge)
+    ts(ta, dv, 1.0, AL.is_ge, -128.0, AL.mult)
+    ts(tc, dv, 0.0, AL.is_equal, float(MARK), AL.mult)
     tt(ta, ta, tc, AL.add)
+    ts(("TRT", 2, 512, 4), ta, 1.0 / 128, AL.mult, float(OWN), AL.min)
     act(("TRT", 3, 512, 4), ("TRT", 2, 512, 4), AF.Copy, scale=-1.0)
     act(("TRT", 0, 512, 4), ta, AF.Copy)
     act(("TRT", 1, 512, 4), ta, AF.Copy, scale=-1.0)
@@ -415,46 +413,42 @@ def rank_program(g, core, T, topo):
 
     for t in range(R):
         tk, ca, pp, pk, hw, hn = "TK%d" % t, "CA%d" % t, "PP%d" % t, "PK%d" % t, "HW%d" % t, "HW%d" % (t + 1)
-        np_, ln = "NP%d" % t, "LN%d" % t
+        np_, ln, final = "NP%d" % t, "LN%d" % t, t + 1 == R
         for s in range(H):
             mm(s, tk, tb + TOK * (H - 1 - s), ca, 0)
-        for s in range(H):
-            score(s)
-        for f, s in ((thr, 0), (thr, 1), (hot, 0), (thr, 2), (hot, 1), (thr, 3)):
+        for f, s in ((score, 0), (score, 1), (score, 2), (thr, 0), (score, 3), (thr, 1), (thr, 2), (hot, 0), (hot, 1), (thr, 3)):
             f(s)
         qz("OC", 0, 128, "OT")
         mm(4, "TRQ", 0, "OC", 0)
         hot(2)
         hot(3)
+        qz("NQ", 0, 128, "NT")
         if t == 0:
             act(("NEW", 64, 512), ("ZT", 0, 448), AF.Copy)
-        scan(("SC", 0, 128), ("RM", 0, 128), ("PS", 2048, 2176), 0.0, AL.mult, AL.max)
-        qz("NQ", 0, 128, "NT")
         mk = ("SC", 31, 128, 32)
-        for i in range(2):
-            ts(("CC", 4 * i, 4 * i + 4), mk, float(BIGW + 128 * i + CAPP - 1), AL.min, float(BIGW + 128 * i), AL.max)
-        for i in range(2):
-            tt(("YF", 20 * i, 20 * i + 20, 5), ("CC", 4 * i, 4 * i + 4), mk, AL.is_equal)
+        scan(("SC", 0, 128), ("RM", 0, 128), ("PS", 2048, 2176), 0.0, AL.mult, AL.max)
         mine(0)
+        for i in range(2):
+            ts(("YF", 20 * i, 20 * i + 20, 5), mk, float(FIRST - 128 * i), AL.is_equal)
+        mine(1)
         tt(("Y", 0, 40), ("YF", 0, 40), ("HI", 0, 40), AL.mult)
         tt(("Y", 40, 80), ("YF", 0, 40), ("LO", 0, 40), AL.mult)
-        mine(1)
+        mine(2)
         qz("YQ", 0, 138, "Y")
         mm(5, "NQ", 0, "YQ", 0, True, False)
         mm(5, "NQ", 0, "YQ", 10, False, True)
-        mine(2)
         mine(3)
         qz("NOQ", 0, 128, "NO")
         mm(6, "NOQ", 0, "YQ", 0, True, False)
         mm(6, "NOQ", 0, "YQ", 10, False, True)
         top2(np_, ("PS", 2560, 2569))
-        ts(("OP%d" % t, 0, 2), (np_, 10, 12), -1.0, AL.mult, float(4 * TOK), AL.add)
-        send([(efar, "aL%d" % t, (np_, 10, 12), [(T.cores[part], (ln, 0, 2))])])
+        ts(("OP%d" % t, 0, 2), (np_, 16, 18), -1.0, AL.mult, float(4 * TOK), AL.add)
+        send([(efar, "aL%d" % t, (np_, 16, 18), [(T.cores[part], (ln, 0, 2))])])
         pick(pp, 0, tk, tb, (lb if half == 0 else TW), "OP%d" % t, 0, 2)
         for k in "cs":
             send([(efar, "aK%d" % t, (pp + k, 0, 32), [(T.cores[part], (tk + k, _land(part), _land(part) + 32))])])
         top2("OW", ("PS", 3072, 3081))
-        n1, n2, n12 = ("OW", 10, 11), ("OW", 11, 12), ("OW", 10, 12)
+        n1, n2, n12 = ("OW", 16, 17), ("OW", 17, 18), ("OW", 16, 18)
         k1z, k2z, k1 = ("KZ", 0, 1), ("KZ", 1, 2), ("KZ", 2, 3)
         b0, b1, b2, c1, c2 = ("BB", 0, 1), ("BB", 1, 2), ("BB", 2, 3), ("CO", 0, 1), ("CO", 1, 2)
         fl = [("FL", i, i + 1) for i in range(12)]
@@ -497,25 +491,34 @@ def rank_program(g, core, T, topo):
         for i in range(2):
             ts((of, 1 + i, 2 + i), ("AA", 1 + i, 2 + i), ("TB", 1 + i, 2 + i), AL.add, ("TU", i, i + 1), AL.add)
 
-        def number():
-            idn = "ID%d" % t
-            ts(("IV", 4, 6), (ln, 0, 2), -1.0, AL.mult, float(ln1), AL.add)
-            if half == 0:
-                tt(("IV", 6, 8), ("IV", 4, 6), ("HF", 0, 2), AL.mult)
-                ts(fl[6], ("IV", 6, 7), fl[5], AL.mult, v2, AL.add)
-                ts(fl[8], ("IV", 6, 7), fl[4], AL.mult, v1, AL.add)
-                ts(fl[9], ("IV", 7, 8), fl[4], AL.mult, fl[6], AL.add)
-            else:
-                ts(fl[6], h1, 0.5, AL.is_lt, v1, AL.mult)
-                tt(("IV", 6, 8), ("IV", 4, 6), ("HF", 0, 2), AL.mult)
-                ts(fl[7], h1, fl[4], AL.mult, v2, AL.add)
-                ts(fl[8], fl[6], ("IV", 6, 7), AL.add)
-                ts(fl[10], h2, 0.5, AL.is_lt, fl[7], AL.mult)
-                ts(fl[9], fl[10], ("IV", 7, 8), AL.add)
-            ts((idn, 0, 2), ("FL", 8, 10), -1.0, AL.add)
+        def lin(out, a, scale, bias):
+            act(out, a, AF.Identity, bias=bias, scale=scale)
 
-        if t + 1 == R:
-            number()
+        u = [("UU", i, i + 1) for i in range(8)]
+
+        def number0():
+            lin(("UU", 0, 2), (ln, 0, 2), -1.0, float(ln1))
+            if half == 1:
+                lin(("UU", 6, 8), ("HF", 0, 2), -1.0, 1.0)
+            lin(u[2], u[0], h1, 0.0)
+            lin(u[3], u[1], h2, 0.0)
+
+        def number1():
+            if half == 0:
+                lin(u[5], u[2], fl[5], v2)
+                lin(("UV", 0, 1), u[2], fl[4], v1)
+                lin(("UV", 1, 2), u[3], fl[4], u[5])
+            else:
+                lin(u[5], h1, fl[4], v2)
+                lin(("UV", 0, 1), v1, u[6], u[2])
+                lin(("UV", 1, 2), u[5], u[7], u[3])
+            lin(("ID%d" % t, 0, 2), ("UV", 0, 2), 1.0, -1.0)
+
+        def store_ids():
+            dma("y", T.ids[:, 32 * t:32 * t + 32], T["ID%d" % t][0:16, 0:2], [("ID%d" % t, 0, 2)], [])
+
+        if final:
+            number0()
         pick(pk, 0, tk, 0, TW, "OF%d" % t, 0, 3)
         for b in range(3):
             mm(b, "E25Q", 128 * b, pk, 0)
@@ -525,7 +528,7 @@ def rank_program(g, core, T, topo):
         ts(("OS%d" % t, 0, 4), ("BQ", 0, 4), ("TT", 1, 2), AL.add)
         w, o, h = ("WN", 0, 128), ("OS%d" % t, 0, 4), ("HC", 0, 64)
         op("s", lambda q, w=w, o=o, h=h: q.activation(view(h), view(w).indirect(view(o)), AF.Copy), [w, o], [h])
-        for f, b in (("h", 0), ("h", 1), ("n", 0), ("h", 2), ("n", 1), ("n", 3), ("n", 2)):
+        for f, b in (("h", 0), ("h", 1), ("n", 0), ("h", 2), ("n", 1), ("n", 2), ("n", 3)):
             c, h = 16 * b, ("PS", 512 * b, 512 * b + 16)
             if f == "h":
                 act(("SS", c, c + 16), ("PS", 512 * b + 16, 512 * b + 32), AF.Copy)
@@ -533,31 +536,35 @@ def rank_program(g, core, T, topo):
             else:
                 tt(("NEW", b, 64, 4), h if b == 3 else ("HB", c, c + 16), ("HC", c, c + 16), AL.add)
         qz(hn, CO, 128, "NEW")
-        if t + 1 < R:
+        if not final:
             for k in "cs":
                 spread(t + 1, k, [efar, enear], hand[k])
             pick("CA%d" % (t + 1), G * rank, hn, 0, 64 + G, "LC", 0, 1)
             for b in range(4):
                 act(("WN", 64 + 16 * b, 80 + 16 * b), ("NEW", b, 64, 4), AF.Copy)
-        else:
-            dma("y", T.ids[:, 32 * t:32 * t + 32], T["ID%d" % t][0:16, 0:2], [("ID%d" % t, 0, 2)], [])
-            i = (hn + "c", CO, CO + G)
-            dma("y", T.oc[:, 0:4 * G], view(i).bitcast(dt.uint8), [i], [])
-            for k in range(4):
-                dma("ys"[k % 2], T.osc[4 * k:4 * k + 4, 0:G], T[hn + "s"][32 * k:32 * k + 4, CO:CO + G], [(hn + "s", CO, CO + G)], [])
         if t == 0:
             qz("WQ", 0, 128, "WT")
-        if t + 1 < R:
+        if not final:
             qz("PK%d" % (t + 1), 0, 144, "ZT")
             qz("HW%d" % (t + 2), 0, 128, "ZT")
         mm(6, "WQ", 0, pk, 0)
-        cp(("YO", 32 * t, 32 * t + 32, 2), ("PS", 3072, 3072 + 16))
-        cp(("YO", 32 * t + 1, 32 * t + 32, 2), ("PS", 3072 + 32, 3072 + 48))
-        if t + 1 < R:
-            number()
+        if final:
+            number1()
+            store_ids()
+        for i in range(2):
+            act(("YO", 32 * t + i, 32 * t + 32, 2), ("PS", 3072 + 32 * i, 3072 + 32 * i + 16), AF.Copy)
+        if final:
+            i = (hn + "c", CO, CO + G)
+            dma("y", T.oc[:, 0:4 * G], view(i).bitcast(dt.uint8), [i], [])
+        else:
+            number0()
+            number1()
             wait("y", ("aC%d" % (t + 1), camec))
-            dma("y", T.ids[:, 32 * t:32 * t + 32], T["ID%d" % t][0:16, 0:2], [("ID%d" % t, 0, 2)], [])
-        dma("y", T.y[:, 32 * t:32 * t + 32], T.YO[:, 32 * t:32 * t + 32], [("YO", 32 * t, 32 * t + 32)], [])
+            store_ids()
+        dma("s" if final else "y", T.y[:, 32 * t:32 * t + 32], T.YO[:, 32 * t:32 * t + 32], [("YO", 32 * t, 32 * t + 32)], [])
+        if final:
+            for k in range(4):
+                dma("ys"[k % 2], T.osc[4 * k:4 * k + 4, 0:G], T[hn + "s"][32 * k:32 * k + 4, CO:CO + G], [(hn + "s", CO, CO + G)], [])
 
     for q in cnt:
         wait("g", (done[q], cnt[q]))

from concourse.bass import DstId, RemoteDMATransfer
from concourse.mybir import dt, AluOpType, AxisListType, ActivationFunctionType

G, TOK, CAPP, R, H = 16, 96, 48, 3, 4
TW = 544
MARK, OWN, STEP = 12288, 80, 64
FIRST = MARK + OWN - (STEP // 2 - (CAPP - STEP // 2))
CO = 48
BY0, BYH = {"c": 0, "s": 1}, {"c": 3, "s": 2}

F32, BF, I32, U16, COD, PLN = "float32", "bfloat16", "int32", "uint16", "float8_e4m3fn_x4", "uint8"
SCRATCH = {"PS": ("psum", [128, 4096], F32)}
SEMAPHORES = ["vd", "sd", "pd", "gd", "sent"]


def _buf(name, n, dtype):
    SCRATCH[name] = ("sbuf", [128, n], dtype)


def _mx(name, n):
    _buf(name + "c", n, COD)
    _buf(name + "s", n, PLN)


for _n, _w in (("CBT", 512), ("X0", 512), ("X12", 768), ("WT", 512), ("ZT", 704), ("TRT", 512), ("E25", 2048), ("THR", 128), ("KP", 128),
               ("KO", 128), ("HI", 40), ("LO", 40), ("OT", 512), ("NT", 512), ("NO", 512), ("YF", 40), ("Y", 552), ("NEW", 512), ("J", 512),
               ("SC", 128)):
    _buf(_n, _w, BF)
for _n, _w in (("RM", 128), ("NEG", 128), ("DV", 128), ("TA", 256), ("QC", 1), ("KZ", 4), ("RB", 512), ("WV", 4), ("OW", 18), ("AA", 4), ("BB", 4),
               ("CO", 2), ("FL", 12), ("TB", 4), ("TU", 2), ("HF", 2), ("TT", 4), ("IV", 4), ("UU", 8), ("UV", 2),
               ("SS", 64), ("HB", 64), ("WN", 128), ("HC", 64), ("BQ", 4), ("YO", 96)):
    _buf(_n, _w, F32)
for _n, _w in (("QI", 1), ("QJ", 1), ("NJ", 6), ("NV", 120), ("RI", 128)):
    _buf(_n, _w, I32)
for _n, _w in (("LI", 6), ("LC", 2)):
    _buf(_n, _w, U16)
for _n, _w in (("XQ0", 128), ("XQ12", 192), ("WQ", 128), ("TRQ", 128), ("E25Q", 512), ("OC", 128), ("NQ", 128), ("NOQ", 128), ("YQ", 138),
               ("HX0", 96), ("HX12", 192)):
    _mx(_n, _w)
for _t in range(R):
    _mx("TK%d" % _t, TW)
    _mx("CA%d" % _t, 128)
    _mx("PP%d" % _t, 32)
    _mx("PK%d" % _t, 144)
    _buf("NP%d" % _t, 18, F32)
    _buf("LN%d" % _t, 2, F32)
    _buf("ID%d" % _t, 2, F32)
    _buf("OP%d" % _t, 2, U16)
    _buf("OF%d" % _t, 4, U16)
    _buf("OS%d" % _t, 4, U16)
    SEMAPHORES += ["aC%d" % _t, "aT%d" % _t, "aL%d" % _t, "aK%d" % _t, "hc%d" % _t, "hs%d" % _t, "gc%d" % _t, "gs%d" % _t]
for _t in range(R + 1):
    _mx("HW%d" % _t, 176)
SEMAPHORES += ["d%d" % _i for _i in range(30)]


def _bits(es):
    return sum(1 << e for e in es)


def _helper_of(core, T, topo, i):
    return [c for c in topo.cores_of(core) if T.rank_of(c) is None and topo.die(c) == topo.die(core)][i]


def _half(r):
    return list(range(H * (r // H), H * (r // H) + H))


def _base(r):
    return 0 if r < H else 32


def _land(r):
    return 4 * TOK + 32 if r < H else 0


def _dst(c, topo):
    a = topo.addr(c)
    return DstId(rid=a[0], pnc=a[1])


def _relay(t):
    return ("Q0", 0) if t == 0 else ("Q12", TOK * (t - 1))


def _far(rank, T, topo):
    n = len(T.cores)
    order = [(rank + i) % n for i in range(1, n)]
    return [r for r in order if topo.chip(T.cores[r]) != topo.chip(T.cores[rank])]


def _near_engines(a, b, far, topo):
    return [e for e in topo.engines(a, b) if e not in topo.engines(a, far)]


def _hand_on(g, core, rank, T, topo, k):
    me = T.cores[rank]
    far = [r for r in _half(rank) if topo.chip(T.cores[r]) != topo.chip(me)]
    es = topo.engines(core, T.cores[far[0]])
    near = _near_engines(me, core, T.cores[far[0]], topo)
    byt = (lambda v: v.bitcast(dt.uint8)) if k == "c" else (lambda v: v)
    n = 0
    for t in range(R):
        g.wait_ge(T.sem["h%s%d" % (k, t)], len(near) if t == 0 else len(near) // 2)
        dsts = []
        for r in far:
            o = _base(r) + TOK * (rank % H)
            dsts.append(byt(T["TK%d%s" % (t, k)][:, o:o + TOK]))
        nm, a = _relay(t)
        g.remote_dma_fused([RemoteDMATransfer(dst_ids=[_dst(T.cores[r], topo) for r in far], dma_engine_mask=_bits(es),
                                              remote_sem=T.sem["aT%d" % t], srcs=[byt(T["HX" + nm[1:] + k][:, a:a + TOK])], dsts=dsts)],
                           local_sem=T.sem.sent)
        n += len(es)
    mate = [r for r in range(len(T.cores)) if r != rank and topo.chip(T.cores[r]) == topo.chip(me)]
    en = _near_engines(core, T.cores[mate[0]], T.cores[far[0]], topo)
    for t in range(1, R):
        last = _far(rank, T, topo)[-BYH[k]:]
        g.wait_ge(T.sem["g%s%d" % (k, t)], len(near))
        v = byt(T["CA%d%s" % (t, k)][:, G * rank:G * rank + G])
        g.remote_dma_fused([RemoteDMATransfer(dst_ids=[_dst(T.cores[r], topo) for r in rs], dma_engine_mask=_bits(e), remote_sem=T.sem["aC%d" % t],
                                              srcs=[v], dsts=[v] * len(rs)) for e, rs in ((es, last), (en, mate))], local_sem=T.sem.sent)
        n += len(es) + len(en)
    g.wait_ge(T.sem.sent, n)


def _first(g, core, rank, T, topo):
    last = _far(rank, T, topo)[-BY0["s"]:]
    es = topo.engines(core, T.cores[last[0]])
    g.wait_ge(T.sem.gs0, len(_near_engines(T.cores[rank], core, T.cores[last[0]], topo)))
    v = T.CA0s[:, G * rank:G * rank + G]
    g.remote_dma_fused([RemoteDMATransfer(dst_ids=[_dst(T.cores[r], topo) for r in last], dma_engine_mask=_bits(es), remote_sem=T.sem.aC0,
                                          srcs=[v], dsts=[v] * len(last))], local_sem=T.sem.sent)
    g.wait_ge(T.sem.sent, len(es))


def rank_program(g, core, T, topo):
    rank = T.rank_of(core)
    if rank is None:
        for r in range(len(T.cores)):
            for i, k in enumerate("cs"):
                if _helper_of(T.cores[r], T, topo, i) == core:
                    _hand_on(g, core, r, T, topo, k)
            if _helper_of(T.cores[r], T, topo, 2) == core:
                _first(g, core, r, T, topo)
        return
    AL, AF, AX = AluOpType, ActivationFunctionType, AxisListType.X
    half, sl = rank // H, rank % H
    part = (rank + H) % (2 * H)
    both = (rank, part)
    tb, lb = _base(rank), _land(rank)
    z = tb + 4 * TOK
    on1, ln1 = (H * TOK + 1, 2 * H * TOK + 1) if half == 0 else (2 * H * TOK + 1, H * TOK + 1)
    eng = {"v": g.vector, "s": g.scalar, "p": g.tensor, "g": g, "y": g.sync}
    done = {"v": "vd", "s": "sd", "p": "pd", "g": "gd"}
    cnt, seen, log, nd = {}, {}, {}, [0]

    def cols(x):
        nm, a, b = x[0], x[1], x[2]
        st = x[3] if len(x) > 3 else 1
        if nm == "PS":
            return nm, frozenset(range(a // 512, (b - 1) // 512 + 1))
        return nm, frozenset(range(a, b, st))

    def view(x):
        st = x[3] if len(x) > 3 else 1
        return T[x[0]][:, x[1]:x[2]] if st == 1 else T[x[0]][:, x[1]:x[2]:st]

    def wait(q, tok):
        if seen.get((q, tok[0]), 0) < tok[1]:
            eng[q].wait_ge(T.sem[tok[0]], tok[1])
            seen[(q, tok[0])] = tok[1]

    def before(q, rd, wr):
        best = {}
        for kind, xs in (("r", rd), ("w", wr)):
            for x in xs:
                nm, cs = cols(x)
                for k, c2, tok, q2 in log.get(nm, []):
                    if (kind == "w" or k == "w") and cs & c2 and not (q == "p" and q2 == "p"):
                        best[tok[0]] = max(best.get(tok[0], 0), tok[1])
        for s in sorted(best):
            wait(q, (s, best[s]))

    def after(q, tok, rd, wr):
        for x in wr:
            nm, cs = cols(x)
            log[nm] = [e for e in log.get(nm, []) if not e[1] <= cs] + [("w", cs, tok, q)]
        for x in rd:
            nm, cs = cols(x)
            log.setdefault(nm, []).append(("r", cs, tok, q))

    def op(q, f, rd, wr):
        before(q, rd, wr)
        cnt[q] = cnt.get(q, 0) + 1
        tok = (done[q], cnt[q])
        f(eng[q]).then_inc(T.sem[tok[0]], 1)
        after(q, tok, rd, wr)
        return tok

    def isap(x):
        return isinstance(x, tuple)

    def ts(out, in0, s1, op0, s2=None, op1=None):
        sc = [view(s) if isap(s) else s for s in (s1, s2)]
        rd = [in0] + [s for s in (s1, s2) if isap(s)]
        if op1 is None:
            return op("v", lambda v: v.tensor_scalar(view(out), view(in0), sc[0], None, op0), rd, [out])
        return op("v", lambda v: v.tensor_scalar(view(out), view(in0), sc[0], sc[1], op0, op1), rd, [out])

    def tt(out, a, b, o):
        return op("v", lambda v: v.tensor_tensor(view(out), view(a), view(b), o), [a, b], [out])

    def cp(out, a):
        return op("v", lambda v: v.tensor_copy(view(out), view(a)), [a], [out])

    def act(out, a, f, bias=0.0, scale=1.0, acc=None):
        rd = [a] + [x for x in (bias, scale) if isap(x)]
        b, c = [view(x) if isap(x) else x for x in (bias, scale)]
        if acc is not None:
            return op("s", lambda s: s.activation(view(out), view(a), f, bias=b, scale=c, accum_out=view(acc)), rd, [out, acc])
        if f == AF.Copy:
            return op("s", lambda s: s.activation(view(out), view(a), f, scale=c), rd, [out])
        return op("s", lambda s: s.activation(view(out), view(a), f, bias=b, scale=c), rd, [out])

    def fill(x, c):
        return op("v", lambda v: v.memset(view(x), c), [], [x])

    def scan(out, d0, d1, ini, o0, o1):
        return op("v", lambda v: v.tensor_tensor_scan(view(out), view(d0), view(d1), ini, o0, o1), [d0, d1], [out])

    def top2(nm, x):
        scan((nm, 0, 17, 2), x, ("NEG", 0, 9), 0.0, AL.max, AL.max)
        scan((nm, 3, 18, 2), (x[0], x[1] + 1, x[2]), (nm, 0, 15, 2), 0.0, AL.max, AL.min)

    def qz(nm, a, n, tile, ta=0):
        oc, os, i = (nm + "c", a, a + n), (nm + "s", a, a + n), (tile, ta, ta + 4 * n)
        return op("v", lambda v: v.quantize_mx(view(oc), view(os), view(i)), [i], [oc, os])

    def mm(bank, st, sa, mv, ma, start=True, stop=True):
        o = ("PS", 512 * bank, 512 * bank + 128)
        a, b = (st + "c", sa, sa + 128), (st + "s", sa, sa + 128)
        c, d = (mv + "c", ma, ma + 128), (mv + "s", ma, ma + 128)
        return op("p", lambda p: p.matmul_mx(view(o), view(a), view(b), view(c), view(d), start, stop), [a, b, c, d], [o])

    def pick(dst, da, src, wa, wb, of, oa, ob):
        n = 16 * (ob - oa)
        o, w, f = (of, oa, ob), (src + "c", wa, wb), (dst + "c", da, da + n)
        op("v", lambda v: v.tensor_copy(view(f).bitcast(dt.uint32), view(w).bitcast(dt.uint32).indirect(view(o))), [w, o], [f])
        w2, f2 = (src + "s", wa, wb), (dst + "s", da, da + n)
        op("s", lambda s: s.activation(view(f2), view(w2).indirect(view(o)), AF.Copy), [w2, o], [f2])

    def dma(q, out, in_, rd, wr):
        before(q, rd, wr)
        tok = ("d%d" % nd[0], 16)
        nd[0] += 1
        eng[q].dma_start(out, in_).then_inc(T.sem[tok[0]], 16)
        after(q, tok, rd, wr)

    def iota(x, pat, base, ch):
        if SCRATCH[x[0]][2] == I32:
            op("g", lambda e: e.iota(view(x), pat, base, ch), [], [x])
        else:
            op("g", lambda e: e.iota(view(x), pat, base, ch, allow_small_or_imprecise_dtypes=True), [], [x])

    def ext(sem, val, xs):
        for x in xs:
            nm, cs = cols(x)
            log.setdefault(nm, []).append(("w", cs, (sem, val), "x"))

    peers = [r for r in range(len(T.cores)) if r != rank]
    near = [r for r in peers if topo.chip(T.cores[r]) == topo.chip(core)]
    far = _far(rank, T, topo)
    efar = topo.engines(core, T.cores[far[0]])
    enear = _near_engines(core, T.cores[near[0]], T.cores[far[0]], topo)
    hn2 = len(enear) // 2
    hand = {"c": _helper_of(core, T, topo, 0), "s": _helper_of(core, T, topo, 1)}
    sent = [0]

    def send(transfers):
        tr, rd = [], []
        for es, sem, src, dsts in transfers:
            code = SCRATCH[src[0]][2] == COD
            b = (lambda v: v.bitcast(dt.uint8)) if code else (lambda v: v)
            tr.append(RemoteDMATransfer(dst_ids=[_dst(c, topo) for c, _ in dsts], dma_engine_mask=_bits(es), remote_sem=T.sem[sem],
                                        srcs=[b(view(src))], dsts=[b(view(x)) for _, x in dsts]))
            rd.append(src)
            sent[0] += len(es)
        before("g", rd, [])
        g.remote_dma_fused(tr, local_sem=T.sem.sent)

    def spread(t, k, es, to):
        src = ("HW%d%s" % (t, k), CO, CO + G)
        x = ("CA%d%s" % (t, k), G * rank, G * rank + G)
        direct = len(far) - (BY0[k] if t == 0 else BYH[k])
        tr = []
        if es[0]:
            tr.append((es[0], "aC%d" % t, src, [(T.cores[r], x) for r in far[:direct]]))
        if es[1]:
            tr.append((es[1], "aC%d" % t if to == "mate" else "g%s%d" % (k, t), src, [(T.cores[near[0]] if to == "mate" else to, x)]))
        send(tr)

    def tokens(t, k, es):
        nm, a = _relay(t)
        src = ("X" + nm + k, a, a + TOK)
        o = tb + TOK * sl
        tr = []
        if es[0]:
            tr.append((es[0], "h%s%d" % (k, t), src, [(hand[k], ("HX" + nm[1:] + k, a, a + TOK))]))
        if es[1]:
            tr.append((es[1], "aT%d" % t, src, [(T.cores[r], ("TK%d%s" % (t, k), o, o + TOK)) for r in near]))
        send(tr)

    dma("y", T.CBT[:, 0:4 * G], T.cb[:], [], [("CBT", 0, 4 * G)])
    dma("s", T.X0[:, 0:4 * TOK], T.x[:, 0:4 * TOK], [], [("X0", 0, 4 * TOK)])
    dma("y", T.X12[:], T.x[:, 4 * TOK:12 * TOK], [], [("X12", 0, 8 * TOK)])
    dma("s", T.WT[:], T.w[:], [], [("WT", 0, 512)])
    iota(("DV", 0, 128), [[1, 128]], 0, -1)
    iota(("QI", 0, 1), [[0, 1]], 0, 1)
    iota(("NJ", 0, 6), [[16, 6]], 0, 0)
    iota(("NV", 0, 40), [[0, 10], [TOK, 4]], TOK, -1)
    fill(("CBT", 4 * G, 512), 0.0)
    fill(("ZT", 0, 704), 0.0)
    for t in range(R):
        qz("TK%d" % t, tb + 4 * TOK, 128, "ZT")
    qz("HW0", 0, 128, "ZT")
    fill(("X0", 4 * TOK, 512), 0.0)
    qz("XQ0", 0, 128, "X0")
    qz("HW0", CO, 128, "CBT")
    for k in "cs":
        tokens(0, k, [enear, []])
    spread(0, "c", [efar, []], None)
    spread(0, "s", [efar, enear], _helper_of(core, T, topo, 2))
    for k in "cs":
        spread(0, k, [[], enear], "mate")
    for k in "cs":
        tokens(0, k, [[], enear])
    qz("XQ12", 0, 2 * TOK, "X12")
    for t in range(1, R):
        for k in "cs":
            tokens(t, k, [enear[hn2:], enear[:hn2]])
    camec = 2 * (len(efar) * len(far) + len(enear) * len(near))
    for t in range(R):
        came = 2 * (len(enear) if t == 0 else hn2) + 2 * len(efar) * len([r for r in _half(rank) if r in far])
        for s in range(H):
            if s != sl:
                ext("aT%d" % t, came, [("TK%d%s" % (t, k), tb + TOK * s, tb + TOK * s + TOK) for k in "cs"])
        for r in peers:
            ext("aC%d" % t, camec, [("CA%d%s" % (t, k), G * r, G * r + G) for k in "cs"])
        ext("aK%d" % t, 2 * len(efar), [("TK%d%s" % (t, k), lb, lb + 32) for k in "cs"])
        ext("aL%d" % t, len(efar), [("LN%d" % t, 0, 2)])

    dv, ta, tc = ("DV", 0, 128), ("TA", 0, 128), ("TA", 128, 256)
    for b in range(4):
        act(("E25", 512 * b, 512 * b + 512), ("ZT", 0, 512), AF.Copy)
    act(("NEG", 0, 128), ("ZT", 0, 128), AF.Identity, bias=-1e29)
    act(("YF", 0, 40), ("ZT", 0, 40), AF.Copy)
    for e in range(2):
        iota(("THR", 64 * e, 64 * e + 64), [[1, G], [1, 4]], G * both[e], 0)
    iota(("KP", 0, 128), [[0, 8], [1, 16]], G * part, 0)
    iota(("RI", 0, 128), [[0, 4], [1, 32]], 0, 0)
    iota(("KO", 0, 128), [[0, 8], [1, 16]], G * rank, 0)
    for e in range(2):
        for i in range(2):
            iota(("THR", 64 * e + 2 + i, 64 * e + 64, 4), [[0, G]], G * (both[e] + i), 0)
    ts(ta, dv, 1.0, AL.is_ge, -128.0, AL.mult)
    ts(tc, dv, 0.0, AL.is_equal, float(MARK), AL.mult)
    tt(ta, ta, tc, AL.add)
    ts(("TRT", 2, 512, 4), ta, 1.0 / 128, AL.mult, float(OWN), AL.min)
    act(("TRT", 3, 512, 4), ("TRT", 2, 512, 4), AF.Copy, scale=-1.0)
    act(("TRT", 0, 512, 4), ta, AF.Copy)
    act(("TRT", 1, 512, 4), ta, AF.Copy, scale=-1.0)
    for b in range(4):
        ts(("E25", 512 * b + b, 512 * b + 512, 4), dv, 0.0, AL.is_equal, 0.25, AL.mult)
    ts(("QJ", 0, 1), ("QI", 0, 1), 15, AL.bitwise_and)
    cp(("QC", 0, 1), ("QJ", 0, 1))
    ts(("LI", 0, 6), ("NJ", 0, 6), ("QC", 0, 1), AL.add)
    ts(("LC", 0, 1), ("QC", 0, 1), float(CO), AL.add)
    pick("CA0", G * rank, "HW0", 0, 64 + G, "LC", 0, 1)
    for t in range(R):
        nm, a = _relay(t)
        pick("TK%d" % t, tb + TOK * sl, "X" + nm, a, a + TOK, "LI", 0, 6)
    ts(("RM", 0, 128), ("RI", 0, 128), 0.5, AL.is_ge)
    fill(("TRT", 4 * TOK, 512), 0.0)
    op("v", lambda v: v.memset(T.TRT[TOK:128, :], 0.0), [], [("TRT", 0, 512)])
    qz("TRQ", 0, 128, "TRT")
    ts(("NV", 40, 80), ("NV", 0, 40), 16.0, AL.add)
    ts(("NV", 80, 120), ("NV", 40, 80), 5, AL.arith_shift_right)
    ts(("HI", 0, 40), ("NV", 80, 120), 32.0, AL.mult)
    tt(("LO", 0, 40), ("NV", 0, 40), ("HI", 0, 40), AL.subtract)
    for i, c in enumerate((lb - z, lb + 16 - z, lb)):
        act(("KZ", i, i + 1), ("QC", 0, 1), AF.Identity, bias=float(c))
    act(("Y", 80, 552), ("ZT", 0, 472), AF.Copy)
    for b in range(4):
        act(("BQ", b, b + 1), ("QC", 0, 1), AF.Identity, bias=float(16 * b))
        act(("WN", 64 + 16 * b, 80 + 16 * b), ("CBT", b, 64, 4), AF.Copy)
    qz("HW1", 0, 128, "ZT")
    qz("PK0", 0, 144, "ZT")
    qz("E25Q", 0, 512, "E25")

    def score(s):
        r = ("RB", 128 * s, 128 * s + 128)
        scan(r, ("PS", 512 * s, 512 * s + 128), ("NEG", 0, 128), -1e29, AL.max, AL.max)
        act(("J", 128 * s, 128 * s + 128), r, AF.Sign, bias=("RB", 128 * s + 127, 128 * s + 128), scale=-1.0, acc=("WV", s, s + 1))

    def thr(s):
        ts(("OT", 128 * s, 128 * s + 128), ("THR", 0, 128), ("WV", s, s + 1), AL.is_le)

    def hot(s):
        ts(("NT", s, 512, 4), ("KP", 0, 128), ("WV", s, s + 1), AL.is_equal)

    def mine(s):
        ts(("NO", s, 512, 4), ("KO", 0, 128), ("WV", s, s + 1), AL.is_equal)

    for t in range(R):
        tk, ca, pp, pk, hw, hn = "TK%d" % t, "CA%d" % t, "PP%d" % t, "PK%d" % t, "HW%d" % t, "HW%d" % (t + 1)
        np_, ln, final = "NP%d" % t, "LN%d" % t, t + 1 == R
        for s in range(H):
            mm(s, tk, tb + TOK * (H - 1 - s), ca, 0)
        for f, s in ((score, 0), (score, 1), (score, 2), (thr, 0), (score, 3), (thr, 1), (thr, 2), (hot, 0), (hot, 1), (thr, 3)):
            f(s)
        qz("OC", 0, 128, "OT")
        mm(4, "TRQ", 0, "OC", 0)
        hot(2)
        hot(3)
        qz("NQ", 0, 128, "NT")
        if t == 0:
            act(("NEW", 64, 512), ("ZT", 0, 448), AF.Copy)
        mk = ("SC", 31, 128, 32)
        scan(("SC", 0, 128), ("RM", 0, 128), ("PS", 2048, 2176), 0.0, AL.mult, AL.max)
        mine(0)
        for i in range(2):
            ts(("YF", 20 * i, 20 * i + 20, 5), mk, float(FIRST - 128 * i), AL.is_equal)
        mine(1)
        tt(("Y", 0, 40), ("YF", 0, 40), ("HI", 0, 40), AL.mult)
        tt(("Y", 40, 80), ("YF", 0, 40), ("LO", 0, 40), AL.mult)
        mine(2)
        qz("YQ", 0, 138, "Y")
        mm(5, "NQ", 0, "YQ", 0, True, False)
        mm(5, "NQ", 0, "YQ", 10, False, True)
        mine(3)
        qz("NOQ", 0, 128, "NO")
        mm(6, "NOQ", 0, "YQ", 0, True, False)
        mm(6, "NOQ", 0, "YQ", 10, False, True)
        top2(np_, ("PS", 2560, 2569))
        ts(("OP%d" % t, 0, 2), (np_, 16, 18), -1.0, AL.mult, float(4 * TOK), AL.add)
        send([(efar, "aL%d" % t, (np_, 16, 18), [(T.cores[part], (ln, 0, 2))])])
        pick(pp, 0, tk, tb, (lb if half == 0 else TW), "OP%d" % t, 0, 2)
        for k in "cs":
            send([(efar, "aK%d" % t, (pp + k, 0, 32), [(T.cores[part], (tk + k, _land(part), _land(part) + 32))])])
        top2("OW", ("PS", 3072, 3081))
        n1, n2, n12 = ("OW", 16, 17), ("OW", 17, 18), ("OW", 16, 18)
        k1z, k2z, k1 = ("KZ", 0, 1), ("KZ", 1, 2), ("KZ", 2, 3)
        b0, b1, b2, c1, c2 = ("BB", 0, 1), ("BB", 1, 2), ("BB", 2, 3), ("CO", 0, 1), ("CO", 1, 2)
        fl = [("FL", i, i + 1) for i in range(12)]
        ts(("AA", 0, 3, 2), n12, -1.0, AL.mult, float(z), AL.add)
        ts(fl[0], n2, 0.5, AL.is_lt, n1, AL.mult)
        if half == 0:
            ts(b0, n1, 0.5, AL.is_lt, k1z, AL.mult)
            ts(fl[1], n2, 0.5, AL.is_lt, k1z, AL.mult)
            ts(("AA", 1, 2), fl[0], -1.0, AL.mult, ("AA", 2, 3), AL.add)
            ts(c1, n1, 0.5, AL.is_lt, 16.0, AL.mult)
            ts(b1, fl[1], fl[0], AL.add)
            ts(b2, fl[1], b0, AL.subtract)
            ts(c2, n1, 0.5, AL.is_lt, k2z, AL.mult)
        else:
            ts(b0, n1, k1z, AL.add)
            ts(b2, n2, n1, AL.subtract)
            ts(("AA", 1, 2), fl[0], -1.0, AL.mult, ("AA", 2, 3), AL.add)
            ts(fl[1], n1, 0.5, AL.is_ge, b0, AL.mult)
            ts(c2, b0, 16.0, AL.add)
            ts(fl[2], fl[1], -1.0, AL.mult, k1, AL.add)
            ts(c1, fl[1], 16.0, AL.add)
            ts(b1, fl[2], ("AA", 1, 2), AL.subtract)
        ts(fl[3], n1, 0.5, AL.is_lt, 64.0, AL.mult)
        v1, v2, v12 = ("IV", 0, 1), ("IV", 1, 2), ("IV", 0, 2)
        ts(("IV", 2, 4), n12, 0.5, AL.is_ge, float(on1), AL.mult)
        if half == 0:
            ts(fl[4], n1, 0.5, AL.is_lt)
            ts(fl[5], n2, 0.5, AL.is_lt, fl[4], AL.subtract)
        tt(v12, ("IV", 2, 4), n12, AL.subtract)
        if half == 1:
            ts(fl[4], v1, v2, AL.subtract)
        for b in range(4):
            mm(7, "E25Q", 128 * b, hw, CO - 16 * b, b == 0, b == 3)
        act(("WN", 0, 64), ("PS", 3584, 3584 + 64), AF.Copy, scale=2.0)
        h1, h2, of = ("HF", 0, 1), ("HF", 1, 2), "OF%d" % t
        ts(("HF", 0, 2), (ln, 0, 2), 0.5, AL.is_ge)
        ts(("TB", 0, 3), ("BB", 0, 3), h1, AL.mult)
        ts(("TU", 0, 2), ("CO", 0, 2), h2, AL.mult)
        ts((of, 0, 1), ("AA", 0, 1), ("TB", 0, 1), AL.add)
        for i in range(2):
            ts((of, 1 + i, 2 + i), ("AA", 1 + i, 2 + i), ("TB", 1 + i, 2 + i), AL.add, ("TU", i, i + 1), AL.add)

        def lin(out, a, scale, bias):
            act(out, a, AF.Identity, bias=bias, scale=scale)

        u = [("UU", i, i + 1) for i in range(8)]

        def number0():
            lin(("UU", 0, 2), (ln, 0, 2), -1.0, float(ln1))
            if half == 1:
                lin(("UU", 6, 8), ("HF", 0, 2), -1.0, 1.0)
            lin(u[2], u[0], h1, 0.0)
            lin(u[3], u[1], h2, 0.0)

        def number1():
            if half == 0:
                lin(u[5], u[2], fl[5], v2)
                lin(("UV", 0, 1), u[2], fl[4], v1)
                lin(("UV", 1, 2), u[3], fl[4], u[5])
            else:
                lin(u[5], h1, fl[4], v2)
                lin(("UV", 0, 1), v1, u[6], u[2])
                lin(("UV", 1, 2), u[5], u[7], u[3])
            lin(("ID%d" % t, 0, 2), ("UV", 0, 2), 1.0, -1.0)

        def store_ids():
            dma("y", T.ids[:, 32 * t:32 * t + 32], T["ID%d" % t][0:16, 0:2], [("ID%d" % t, 0, 2)], [])

        if final:
            number0()
        pick(pk, 0, tk, 0, TW, "OF%d" % t, 0, 3)
        for b in range(3):
            mm(b, "E25Q", 128 * b, pk, 0)
        mm(3, "E25Q", 384, pk, 16, True, False)
        mm(3, "E25Q", 384, pk, 0, False, True)
        ts(("TT", 1, 2), h1, 0.5, AL.is_lt, fl[3], AL.mult)
        ts(("OS%d" % t, 0, 4), ("BQ", 0, 4), ("TT", 1, 2), AL.add)
        w, o, h = ("WN", 0, 128), ("OS%d" % t, 0, 4), ("HC", 0, 64)
        op("s", lambda q, w=w, o=o, h=h: q.activation(view(h), view(w).indirect(view(o)), AF.Copy), [w, o], [h])
        for f, b in (("h", 0), ("h", 1), ("n", 0), ("h", 2), ("n", 1), ("n", 2), ("n", 3)):
            c, h = 16 * b, ("PS", 512 * b, 512 * b + 16)
            if f == "h":
                act(("SS", c, c + 16), ("PS", 512 * b + 16, 512 * b + 32), AF.Copy)
                tt(("HB", c, c + 16), h, ("SS", c, c + 16), AL.add)
            else:
                tt(("NEW", b, 64, 4), h if b == 3 else ("HB", c, c + 16), ("HC", c, c + 16), AL.add)
        qz(hn, CO, 128, "NEW")
        if not final:
            for k in "cs":
                spread(t + 1, k, [efar, enear], hand[k])
            pick("CA%d" % (t + 1), G * rank, hn, 0, 64 + G, "LC", 0, 1)
            for b in range(4):
                act(("WN", 64 + 16 * b, 80 + 16 * b), ("NEW", b, 64, 4), AF.Copy)
        if t == 0:
            qz("WQ", 0, 128, "WT")
        if not final:
            qz("PK%d" % (t + 1), 0, 144, "ZT")
            qz("HW%d" % (t + 2), 0, 128, "ZT")
        mm(6, "WQ", 0, pk, 0)
        if final:
            number1()
            store_ids()
        for i in range(2):
            act(("YO", 32 * t + i, 32 * t + 32, 2), ("PS", 3072 + 32 * i, 3072 + 32 * i + 16), AF.Copy)
        if final:
            i = (hn + "c", CO, CO + G)
            dma("y", T.oc[:, 0:4 * G], view(i).bitcast(dt.uint8), [i], [])
        else:
            number0()
            number1()
            wait("y", ("aC%d" % (t + 1), camec))
            store_ids()
        dma("s" if final else "y", T.y[:, 32 * t:32 * t + 32], T.YO[:, 32 * t:32 * t + 32], [("YO", 32 * t, 32 * t + 32)], [])
        if final:
            for k in range(4):
                dma("ys"[k % 2], T.osc[4 * k:4 * k + 4, 0:G], T[hn + "s"][32 * k:32 * k + 4, CO:CO + G], [(hn + "s", CO, CO + G)], [])

    for q in cnt:
        wait("g", (done[q], cnt[q]))
    for i in range(nd[0]):
        wait("g", ("d%d" % i, 16))
    g.wait_ge(T.sem.sent, sent[0])
